import numpy as np
import ml_dtypes


def mxq(x, axis, fmt="e4m3"):
    dtype, down = {"e4m3": (ml_dtypes.float8_e4m3fn, 7), "e5m2": (ml_dtypes.float8_e5m2, 14)}[fmt]
    v = np.moveaxis(np.asarray(x, np.float32).astype(ml_dtypes.bfloat16).astype(np.float64), axis, -1)
    blocks = v.reshape(v.shape[:-1] + (-1, 32))
    amax = np.abs(blocks).max(-1, keepdims=True)
    byte = np.maximum(np.where(amax > 0, np.frexp(amax)[1] - 1 + 127, 0) - down, 1)
    scale = np.exp2(byte - 127.0)
    codes = (blocks / scale).astype(np.float32).astype(dtype).astype(np.float64)
    return np.moveaxis((codes * scale).reshape(v.shape), -1, axis)


WIDE = False


def mx_kscale(k):
    if not WIDE:
        return np.ones(k)
    levels = np.array([10, -10, 5, -5, 0])
    if k % 512:
        return np.exp2(np.random.permutation(np.resize(levels, k // 32))).repeat(32)
    a = np.empty((k // 512, 16))
    for p in range(k // 512):
        a[p, :8] = np.random.permutation(np.resize(levels, 8))
        for g in range(8):
            far = levels[np.abs(levels - a[p, g]) >= 10]
            a[p, g + 8] = far[np.random.randint(len(far))]
    return np.exp2(a.ravel()).repeat(32)


BF16 = ml_dtypes.bfloat16


def bf(x):
    return np.asarray(x, np.float32).astype(BF16)


def f64(x):
    return np.asarray(x).astype(np.float64)

def planes(Y):
    n, m = Y.shape
    b = f64(bf(Y)).reshape(n // 32, 32, m)
    amax = np.abs(b).max(1)
    byte = np.clip(np.where(amax > 0, np.frexp(amax)[1] - 1 + 127 - 7, 1), 1, 254)
    codes = (b * np.exp2(127.0 - byte)[:, None, :]).reshape(n, m).astype(np.float32).astype(ml_dtypes.float8_e4m3fn).view(np.uint8)
    words = codes.reshape(n // 512, 128, 4, m).transpose(0, 1, 3, 2)
    return np.ascontiguousarray(words), np.ascontiguousarray(byte.astype(np.uint8).reshape(n // 512, 16, m))


NB, T, D, N, TWO = 128, 8, 1024, 1024, 2


def setup_inputs():
    s, t = mx_kscale(D), mx_kscale(N)
    return {"u": bf(np.random.standard_normal((NB, T, D)) * s),
            "b": bf(np.random.standard_normal((TWO, D, N)) / np.sqrt(D) / s[None, :, None]),
            "nu": bf(np.random.uniform(-2.0, 0.0, N)),
            "theta": bf(np.random.uniform(0.0, 3.0, N)),
            "gamma": bf(np.random.uniform(0.5, 1.0, N) * t),
            "c": bf(np.random.standard_normal((TWO, N, D)) / np.sqrt(N) / t[None, :, None]),
            "d": bf(np.random.standard_normal(D) * 0.5 / s)}


def diagonal_eigenvalues(nu, theta):
    m = np.exp(-np.exp(nu))
    return m * np.cos(theta), m * np.sin(theta)


def core(u, b, nu, theta, gamma, c, d):
    u, b, nu, theta, gamma, c, d = f64(u), f64(b), f64(nu), f64(theta), f64(gamma), f64(c), f64(d)
    uq = mxq(u, 2, "e4m3")
    ar = uq @ mxq(b[0], 0, "e4m3")
    ai = uq @ mxq(b[1], 0, "e4m3")
    ar = ar * gamma
    ai = ai * gamma

    lr, li = diagonal_eigenvalues(nu, theta)

    hr = np.zeros((u.shape[0], nu.shape[0]))
    hi = np.zeros((u.shape[0], nu.shape[0]))
    real_states = []
    imag_states = []
    for step in range(T):
        hr_new = lr * hr - li * hi + ar[:, step]
        hi_new = lr * hi + li * hr + ai[:, step]
        real_states.append(hr_new)
        imag_states.append(hi_new)
        hr, hi = hr_new, hi_new
    hrs = np.stack(real_states, axis=1)
    his = np.stack(imag_states, axis=1)

    y = (mxq(hrs, 2, "e4m3") @ mxq(c[0], 0, "e4m3")) - (mxq(his, 2, "e4m3") @ mxq(c[1], 0, "e4m3"))

    y = y + d * u
    return y


def reference(u, b, nu, theta, gamma, c, d):
    R_out = core(u, b, nu, theta, gamma, c, d)
    words, scales = planes(np.moveaxis(R_out, 2, 0).reshape(1024, -1))
    return R_out, words, scales

@@ -1,0 +1,404 @@
+import math
+from contextlib import ExitStack
+
+import concourse.mybir as mybir
+from concourse.masks import make_identity
+
+F32 = mybir.dt.float32
+BF16 = mybir.dt.bfloat16
+I32 = mybir.dt.int32
+U32 = mybir.dt.uint32
+U8 = mybir.dt.uint8
+FP8X4 = mybir.dt.float8_e4m3fn_x4
+ALU = mybir.AluOpType
+ACT = mybir.ActivationFunctionType
+
+NB, T, D, N = 128, 8, 1024, 1024
+P = 128
+FLOPS = 4 * 2 * NB * T * D * N
+
+CHUNKS = ((0, 1), (2, 3), (4, 5), (6,), (7,))
+
+
+def tile_linearrecurrentunitcomplexeightstep_x1_kernel(tc, u, b, nu, theta, gamma, c, d, out_0, out_1, out_2):
+    nc = tc.nc
+    with ExitStack() as ctx:
+        const = ctx.enter_context(tc.tile_pool(name="const", bufs=1))
+        pool = ctx.enter_context(tc.tile_pool(name="work", bufs=1))
+        psum = ctx.enter_context(tc.psum_pool(name="psum", bufs=1))
+
+        v4 = const.tile([P, 1024], BF16, name="v4", align_bytes=64)
+        v4p = const.tile([P, 1024], BF16, name="v4p", align_bytes=64)
+        nc.vector.memset(v4[:], 0.0)
+        nc.gpsimd.memset(v4p[:], 0.0)
+        ident32 = const.tile([P, P], F32, name="ident32")
+        make_identity(nc, ident32[:])
+        ident16 = const.tile([P, P], BF16, name="ident16")
+        nc.gpsimd.tensor_copy(out=ident16[:], in_=ident32[:])
+
+        u_nat = {}
+
+        def load_u(ch):
+            w = len(CHUNKS[ch])
+            t0 = CHUNKS[ch][0]
+            u_nat[ch] = pool.tile([P, w, D], BF16, name="u_nat", tag="u_nat", bufs=3, align_bytes=64)
+            nc.sync.dma_start(out=u_nat[ch][:], in_=u[:, t0:t0 + w, :])
+
+        raw = {}
+
+        def load_b(part, g, G):
+            raw["b", part, g, G] = pool.tile([P, 4, 512], BF16, name="raw", tag="raw", bufs=8, align_bytes=64)
+            nc.sync.dma_start(
+                out=raw["b", part, g, G][:],
+                in_=b[part, 512 * g:512 * g + 512, 512 * G:512 * G + 512].rearrange("(p j) w -> p j w", j=4))
+
+        def load_c(part, G, g):
+            raw["c", part, G, g] = pool.tile([P, 4, 512], BF16, name="raw", tag="raw", bufs=8, align_bytes=64)
+            for j in range(4):
+                nc.sync.dma_start(
+                    out=raw["c", part, G, g][:, j, :],
+                    in_=c[part, 512 * G:512 * G + 512, 512 * g:512 * g + 512].rearrange("(q j i) w -> j q i w", j=4, i=8)[j])
+
+        for i, vec in enumerate((nu, theta, gamma, d)):
+            nc.scalar.dma_start(out=v4[i:i + 1, :], in_=vec.unsqueeze(0))
+        load_b(0, 0, 0)
+        load_b(0, 1, 0)
+        load_u(0)
+        load_b(1, 0, 0)
+        load_b(1, 1, 0)
+        for part in range(2):
+            for g in range(2):
+                load_b(part, g, 1)
+        load_u(1)
+        load_u(2)
+
+        vecs = const.tile([P, 8, 4], F32, name="vecs")
+        lam = const.tile([P, 6, 8], F32, name="lam")
+
+        def constants():
+            nc.vector.tensor_copy(
+                out=v4p[0:4, :].rearrange("p (G t q i) -> p G q t i", G=2, t=4, q=16),
+                in_=v4[0:4, :].rearrange("p (G q t i) -> p G q t i", G=2, t=4, q=16))
+            vp = psum.tile([P, 8, P], BF16, name="vp", tag="tr", bufs=2)
+            for k in range(8):
+                nc.tensor.transpose(vp[:, k, :], v4p[:, P * k:P * k + P], ident16[:])
+            nc.vector.tensor_copy(out=vecs[:, :, 0:3], in_=vp[:, :, 0:3])
+            dp = psum.tile([P, 8, P], BF16, name="dp", tag="tr", bufs=2)
+            for k in range(8):
+                g, t = divmod(k, 4)
+                nc.tensor.transpose(dp[:, k, :], v4[:, 512 * g + t:512 * g + 512:4], ident16[:])
+            nc.vector.tensor_copy(out=vecs[:, :, 3:4], in_=dp[:, :, 3:4])
+
+            tmp = const.tile([P, 5, 8], F32, name="tmp")
+            nc.scalar.activation(out=tmp[:, 0, :], in_=vecs[:, :, 0], func=ACT.Exp)
+            nc.scalar.activation(out=tmp[:, 1, :], in_=tmp[:, 0, :], func=ACT.Exp, scale=-1.0)
+            nc.vector.tensor_scalar(out=tmp[:, 2, :], in0=vecs[:, :, 1], scalar1=-1.0, scalar2=math.pi / 2, op0=ALU.mult, op1=ALU.add)
+            nc.scalar.activation(out=tmp[:, 3, :], in_=vecs[:, :, 1], func=ACT.Sin)
+            nc.scalar.activation(out=tmp[:, 4, :], in_=tmp[:, 2, :], func=ACT.Sin)
+            nc.vector.tensor_copy(out=lam[:, 3, :], in_=vecs[:, :, 2])
+            nc.vector.tensor_copy(out=lam[:, 4, :], in_=vecs[:, :, 3])
+            nc.vector.tensor_tensor(out=lam[:, 0, :], in0=tmp[:, 1, :], in1=tmp[:, 4, :], op=ALU.mult)
+            nc.vector.tensor_tensor(out=lam[:, 1, :], in0=tmp[:, 1, :], in1=tmp[:, 3, :], op=ALU.mult)
+            nc.vector.tensor_scalar(out=lam[:, 2, :], in0=lam[:, 1, :], scalar1=-1.0, scalar2=None, op0=ALU.mult)
+
+        LR, LI, NLI, GAM, DD = range(5)
+
+        def col(which, k):
+            return lam[:, which, k:k + 1]
+
+        grouped = {}
+        codes = {}
+        scales = {}
+
+        def interleave(eng, key):
+            grouped[key] = pool.tile([P, 2048], BF16, name="grouped", tag="grouped", bufs=3, align_bytes=64)
+            if key[0] == "b":
+                out = grouped[key][:].rearrange("p (t q i j) -> p q t i j", t=4, q=16, i=8)
+                in_ = raw[key][:].rearrange("p j (q t i) -> p q t i j", t=4, i=8)
+            else:
+                out = grouped[key][:].rearrange("p (t m j) -> p m j t", t=4, j=4)
+                in_ = raw[key][:].rearrange("p j (m t) -> p m j t", t=4)
+            if eng == "V":
+                nc.vector.tensor_copy(out=out, in_=in_)
+            else:
+                nc.scalar.copy(out=out, in_=in_)
+
+        def quant_w(key):
+            codes[key] = const.tile([P, 512], U32, name="wc_" + "_".join([str(k) for k in key]), align_bytes=64)
+            scales[key] = const.tile([P, 512], U8, name="ws_" + "_".join([str(k) for k in key]), align_bytes=64)
+            nc.vector.quantize_mx(out=codes[key][:].bitcast(FP8X4), scales=scales[key][:], in_=grouped[key][:])
+
+        ug = {}
+        uq = {}
+        us = {}
+
+        def u_transpose(ch):
+            w = len(CHUNKS[ch])
+            ug[ch] = const.tile([P, 2, w * P, 4], BF16, name="ug%d" % ch, align_bytes=64)
+            words = u_nat[ch][:].rearrange("p w k -> p (w k)").bitcast(F32)
+            for s in range(w):
+                bank = psum.tile([P, 2, 2, P], F32, name="xt", tag="tr", bufs=2)
+                for g in range(2):
+                    for e in range(2):
+                        lo = 512 * s + 256 * g
+                        nc.tensor.transpose(bank[:, g, e, :], words[:, lo + e:lo + 256:2], ident32[:])
+                nc.scalar.copy(
+                    out=ug[ch][:, :, P * s:P * s + P, :].rearrange("p g n j -> p g (n j)").bitcast(F32).rearrange("p g (n e) -> p g n e", e=2),
+                    in_=bank[:].rearrange("p g e n -> p g n e"))
+
+        def u_quant(ch):
+            w = len(CHUNKS[ch])
+            uq[ch] = pool.tile([P, 2 * w * P], U32, name="uq", tag="uq", bufs=2, align_bytes=64)
+            us[ch] = pool.tile([P, 2 * w * P], U8, name="us", tag="us", bufs=2, align_bytes=64)
+            nc.vector.quantize_mx(out=uq[ch][:].bitcast(FP8X4), scales=us[ch][:], in_=ug[ch][:].rearrange("p g n j -> p (g n j)"))
+
+        state = {}
+        acc = {}
+
+        def stage1(ch, n):
+            w = len(CHUNKS[ch])
+            G, t = divmod(n, 4)
+            acc[ch, n] = psum.tile([P, 2, w * P], F32, name="acc", tag="acc", bufs=3)
+            for part in range(2):
+                for g in range(2):
+                    key = ("b", part, g, G)
+                    nc.tensor.matmul_mx(
+                        out=acc[ch, n][:, part, :],
+                        lhsT=codes[key][:, P * t:P * t + P].bitcast(FP8X4), lhsT_scale=scales[key][:, P * t:P * t + P],
+                        rhs=uq[ch][:, w * P * g:w * P * (g + 1)].bitcast(FP8X4), rhs_scale=us[ch][:, w * P * g:w * P * (g + 1)],
+                        start=(g == 0), stop=(g == 1))
+
+        def drain(ch, n):
+            w = len(CHUNKS[ch])
+            G, t = divmod(n, 4)
+            if (ch, G) not in state:
+                state[ch, G] = pool.tile([P, 4, 2, w * P], F32, name="state", tag="state", bufs=4, align_bytes=64)
+            nc.scalar.activation(out=state[ch, G][:, t, :, :], in_=acc[ch, n][:], func=ACT.Copy, scale=col(GAM, n))
+
+        def project(ch, G):
+            for t in range(4):
+                stage1(ch, 4 * G + t)
+                drain(ch, 4 * G + t)
+
+        def recur(ch, G):
+            for s in range(len(CHUNKS[ch])):
+                if CHUNKS[ch][s] == 0:
+                    continue
+                if s > 0:
+                    prev = state[ch, G][:, :, :, P * (s - 1):P * s]
+                else:
+                    wp = len(CHUNKS[ch - 1])
+                    prev = state[ch - 1, G][:, :, :, P * (wp - 1):P * wp]
+                cur = state[ch, G][:, :, :, P * s:P * s + P]
+                for t in range(4):
+                    n = 4 * G + t
+                    nc.vector.scalar_tensor_tensor(out=cur[:, t, 0, :], in0=prev[:, t, 1, :], scalar=col(NLI, n), in1=cur[:, t, 0, :], op0=ALU.mult, op1=ALU.add)
+                    nc.vector.scalar_tensor_tensor(out=cur[:, t, 1, :], in0=prev[:, t, 0, :], scalar=col(LI, n), in1=cur[:, t, 1, :], op0=ALU.mult, op1=ALU.add)
+                for t in range(4):
+                    nc.vector.scalar_tensor_tensor(out=cur[:, t, :, :], in0=prev[:, t, :, :], scalar=col(LR, 4 * G + t), in1=cur[:, t, :, :], op0=ALU.mult, op1=ALU.add)
+
+        hb = {}
+        hq = {}
+        hs = {}
+
+        def h_copy(eng, ch, G, part):
+            w = len(CHUNKS[ch])
+            if (ch, G) not in hb:
+                hb[ch, G] = pool.tile([P, 2, w * P, 4], BF16, name="hb", tag="hb", bufs=3, align_bytes=64)
+            out = hb[ch, G][:, part, :, :].rearrange("p (c i) t -> p c t i", i=4)
+            in_ = state[ch, G][:, :, part, :].rearrange("p t (c i) -> p c t i", i=4)
+            sign = 1.0 - 2.0 * part
+            if eng == "V":
+                nc.vector.tensor_scalar(out=out, in0=in_, scalar1=sign, scalar2=None, op0=ALU.mult)
+            else:
+                nc.scalar.activation(out=out, in_=in_, func=ACT.Copy, scale=sign)
+
+        def h_quant(ch, G):
+            w = len(CHUNKS[ch])
+            hq[ch, G] = pool.tile([P, 2 * w * P], U32, name="hq", tag="hq", bufs=4, align_bytes=64)
+            hs[ch, G] = pool.tile([P, 2 * w * P], U8, name="hs", tag="hs", bufs=4, align_bytes=64)
+            nc.vector.quantize_mx(out=hq[ch, G][:].bitcast(FP8X4), scales=hs[ch, G][:], in_=hb[ch, G][:].rearrange("p r n t -> p (r n t)"))
+
+        yp = {}
+        ysb = {}
+        yb = [const.tile([P, NB, T, 4], BF16, name="yb%d" % g, align_bytes=64) for g in range(2)]
+
+        def stage2(ch, k):
+            w = len(CHUNKS[ch])
+            per = 4 // w
+            if k % per == 0:
+                yp[ch, k // per] = psum.tile([P, per, w * P], F32, name="yp", tag="yp", bufs=3)
+            g, t = divmod(k, 4)
+            for i in range(4):
+                G, part = divmod(i, 2)
+                key = ("c", part, G, g)
+                nc.tensor.matmul_mx(
+                    out=yp[ch, k // per][:, k % per, :],
+                    lhsT=codes[key][:, P * t:P * t + P].bitcast(FP8X4), lhsT_scale=scales[key][:, P * t:P * t + P],
+                    rhs=hq[ch, G][:, w * P * part:w * P * (part + 1)].bitcast(FP8X4), rhs_scale=hs[ch, G][:, w * P * part:w * P * (part + 1)],
+                    start=(i == 0), stop=(i == 3))
+
+        def skip_add(ch, k):
+            w = len(CHUNKS[ch])
+            per = 4 // w
+            g, t = divmod(k, 4)
+            if (ch, g) not in ysb:
+                ysb[ch, g] = pool.tile([P, 4, w * P], F32, name="ysb", tag="ysb", bufs=4, align_bytes=64)
+            nc.vector.scalar_tensor_tensor(
+                out=ysb[ch, g][:, t, :], in0=ug[ch][:, g, :, t], scalar=col(DD, k), in1=yp[ch, k // per][:, k % per, :], op0=ALU.mult, op1=ALU.add)
+
+        def y_round(eng, ch, g):
+            w = len(CHUNKS[ch])
+            t0 = CHUNKS[ch][0]
+            out = yb[g][:, :, t0:t0 + w, :].rearrange("p (c i) s t -> p c s t i", i=4)
+            in_ = ysb[ch, g][:].rearrange("p t (s c i) -> p c s t i", s=w, i=4)
+            if eng == "V":
+                nc.vector.tensor_copy(out=out, in_=in_)
+            else:
+                nc.scalar.copy(out=out, in_=in_)
+
+        osb = {}
+
+        def y_store(eng, ch, g, s):
+            w = len(CHUNKS[ch])
+            t = CHUNKS[ch][s]
+            bank = psum.tile([P, 4, P], F32, name="ot", tag="tr", bufs=2)
+            for k in range(4):
+                nc.tensor.transpose(bank[:, k, :], ysb[ch, g][:, k, P * s:P * s + P], ident32[:])
+            if (ch, s) not in osb:
+                osb[ch, s] = pool.tile([P, D], F32, name="osb", tag="osb", bufs=3, align_bytes=64)
+            out = osb[ch, s][:, 512 * g:512 * g + 512].rearrange("p (m t) -> p m t", t=4)
+            in_ = bank[:].rearrange("p t m -> p m t")
+            if eng == "V":
+                nc.vector.tensor_copy(out=out, in_=in_)
+            else:
+                nc.scalar.copy(out=out, in_=in_)
+            if g == 1:
+                nc.sync.dma_start(out=out_0[:, t, :], in_=osb[ch, s][:])
+
+        n_ch = len(CHUNKS)
+        ckeys = [("c", part, G, g) for G in range(2) for part in range(2) for g in range(2)]
+
+        def bk(G, i):
+            return ("b", i // 2, i % 2, G)
+
+        def cload(i):
+            load_c(ckeys[i][1], ckeys[i][2], ckeys[i][3])
+
+        def h_round(ch, G, engs="SS"):
+            h_copy(engs[0], ch, G, 0)
+            h_copy(engs[1], ch, G, 1)
+
+        def back(ch, g):
+            for j in range(4):
+                skip_add(ch, 4 * g + j)
+
+        def out(ch, g, engs="SSS"):
+            y_round(engs[0], ch, g)
+            for s in range(len(CHUNKS[ch])):
+                y_store(engs[1 + s], ch, g, s)
+
+        interleave("V", bk(0, 0))
+        interleave("S", bk(0, 1))
+        constants()
+        quant_w(bk(0, 0))
+        u_transpose(0)
+        interleave("V", bk(0, 2))
+        u_quant(0)
+        quant_w(bk(0, 1))
+        interleave("S", bk(0, 3))
+        quant_w(bk(0, 2))
+        load_u(3)
+        for i in range(4):
+            cload(i)
+        interleave("V", bk(1, 0))
+        quant_w(bk(0, 3))
+        project(0, 0)
+        quant_w(bk(1, 0))
+        interleave("V", bk(1, 1))
+        interleave("S", bk(1, 2))
+        recur(0, 0)
+        quant_w(bk(1, 1))
+        interleave("V", bk(1, 3))
+        quant_w(bk(1, 2))
+        u_transpose(1)
+        quant_w(bk(1, 3))
+        u_quant(1)
+        for i in range(4):
+            cload(4 + i)
+        load_u(4)
+        h_round(0, 0)
+        project(0, 1)
+        project(1, 0)
+        interleave("V", ckeys[0])
+        recur(0, 1)
+        quant_w(ckeys[0])
+        h_quant(0, 0)
+        interleave("S", ckeys[1])
+        interleave("V", ckeys[2])
+        recur(1, 0)
+        quant_w(ckeys[2])
+        h_round(0, 1)
+        project(1, 1)
+        u_transpose(2)
+        quant_w(ckeys[1])
+        interleave("V", ckeys[3])
+        u_quant(2)
+        quant_w(ckeys[3])
+        h_round(1, 0)
+        interleave("V", ckeys[4])
+        recur(1, 1)
+        quant_w(ckeys[4])
+        h_quant(0, 1)
+        interleave("S", ckeys[5])
+        h_quant(1, 0)
+        interleave("V", ckeys[6])
+        project(2, 0)
+        quant_w(ckeys[5])
+        quant_w(ckeys[6])
+        interleave("V", ckeys[7])
+        recur(2, 0)
+        quant_w(ckeys[7])
+        for k in range(8):
+            stage2(0, k)
+        h_round(1, 1)
+        back(0, 0)
+        back(0, 1)
+        for k in range(2, n_ch):
+            project(k, 1)
+            h_round(k, 0)
+            h_quant(k - 1, 1)
+            out(k - 2, 0)
+            for j in range(8):
+                stage2(k - 1, j)
+            recur(k, 1)
+            if k + 1 < n_ch:
+                u_transpose(k + 1)
+                u_quant(k + 1)
+                project(k + 1, 0)
+            h_quant(k, 0)
+            out(k - 2, 1)
+            back(k - 1, 0)
+            back(k - 1, 1)
+            h_round(k, 1)
+            if k + 1 < n_ch:
+                recur(k + 1, 0)
+        h_quant(n_ch - 1, 1)
+        out(n_ch - 2, 0)
+        for j in range(8):
+            stage2(n_ch - 1, j)
+        out(n_ch - 2, 1)
+        back(n_ch - 1, 0)
+        out(n_ch - 1, 0)
+        back(n_ch - 1, 1)
+        out(n_ch - 1, 1)
+
+        ysc = const.tile([P, 2, 1024], U8, name="ysc", align_bytes=64)
+        for g in range(2):
+            yq = const.tile([P, 1024], U32, name="yq%d" % g, align_bytes=64)
+            nc.vector.quantize_mx(out=yq[:].bitcast(FP8X4), scales=ysc[:, g, :], in_=yb[g][:].rearrange("p n s t -> p (n s t)"))
+            nc.sync.dma_start(out=out_1[g].rearrange("p m t -> p (m t)").bitcast(I32), in_=yq[:].bitcast(I32))
+        for q in range(4):
+            nc.sync.dma_start(
+                out=out_2[:, 4 * q:4 * q + 4, :].bitcast(I32).rearrange("g r m -> r g m"),
+                in_=ysc[32 * q:32 * q + 4, :, :].bitcast(I32))

@@ -29,6 +29,9 @@ def tile_linearrecurrentunitcomplexeightstep_x1_kernel(tc, u, b, nu, theta, gamm
 
         v4 = const.tile([P, 1024], BF16, name="v4", align_bytes=64)
         v4p = const.tile([P, 1024], BF16, name="v4p", align_bytes=64)
+        warm = const.tile([P, 2], F32, name="warm")
+        nc.vector.memset(warm[:], 0.0)
+        nc.scalar.activation(out=warm[:, 1:2], in_=warm[:, 0:1], func=ACT.Exp)
         nc.vector.memset(v4[:], 0.0)
         nc.gpsimd.memset(v4p[:], 0.0)
         ident32 = const.tile([P, P], F32, name="ident32")
@@ -41,23 +44,23 @@ def tile_linearrecurrentunitcomplexeightstep_x1_kernel(tc, u, b, nu, theta, gamm
         def load_u(ch):
             w = len(CHUNKS[ch])
             t0 = CHUNKS[ch][0]
-            u_nat[ch] = pool.tile([P, w, D], BF16, name="u_nat", tag="u_nat", bufs=3, align_bytes=64)
+            u_nat[ch] = pool.tile([P, w, D], BF16, name="u_nat", tag="u_nat", bufs=2, align_bytes=64)
             nc.sync.dma_start(out=u_nat[ch][:], in_=u[:, t0:t0 + w, :])
 
         raw = {}
 
         def load_b(part, g, G):
-            raw["b", part, g, G] = pool.tile([P, 4, 512], BF16, name="raw", tag="raw", bufs=8, align_bytes=64)
+            raw["b", part, g, G] = pool.tile([P, 4, 512], BF16, name="raw_b", tag="raw_b", bufs=5, align_bytes=64)
             nc.sync.dma_start(
                 out=raw["b", part, g, G][:],
                 in_=b[part, 512 * g:512 * g + 512, 512 * G:512 * G + 512].rearrange("(p j) w -> p j w", j=4))
 
-        def load_c(part, G, g):
-            raw["c", part, G, g] = pool.tile([P, 4, 512], BF16, name="raw", tag="raw", bufs=8, align_bytes=64)
+        def load_c(part, G):
+            raw["c", part, G] = pool.tile([P, 4, 1024], BF16, name="raw_c", tag="raw_c", bufs=2, align_bytes=64)
             for j in range(4):
                 nc.sync.dma_start(
-                    out=raw["c", part, G, g][:, j, :],
-                    in_=c[part, 512 * G:512 * G + 512, 512 * g:512 * g + 512].rearrange("(q j i) w -> j q i w", j=4, i=8)[j])
+                    out=raw["c", part, G][:, j, :],
+                    in_=c[part, 512 * G:512 * G + 512, :].rearrange("(q j i) w -> j q i w", j=4, i=8)[j])
 
         for i, vec in enumerate((nu, theta, gamma, d)):
             nc.scalar.dma_start(out=v4[i:i + 1, :], in_=vec.unsqueeze(0))
@@ -70,6 +73,8 @@ def tile_linearrecurrentunitcomplexeightstep_x1_kernel(tc, u, b, nu, theta, gamm
             for g in range(2):
                 load_b(part, g, 1)
         load_u(1)
+        load_c(0, 0)
+        load_c(1, 0)
         load_u(2)
 
         vecs = const.tile([P, 8, 4], F32, name="vecs")
@@ -112,12 +117,13 @@ def tile_linearrecurrentunitcomplexeightstep_x1_kernel(tc, u, b, nu, theta, gamm
 
         def interleave(eng, key):
             grouped[key] = pool.tile([P, 2048], BF16, name="grouped", tag="grouped", bufs=3, align_bytes=64)
+            half = raw[key][:] if key[0] == "b" else raw[key[:3]][:, :, 512 * key[3]:512 * key[3] + 512]
             if key[0] == "b":
                 out = grouped[key][:].rearrange("p (t q i j) -> p q t i j", t=4, q=16, i=8)
-                in_ = raw[key][:].rearrange("p j (q t i) -> p q t i j", t=4, i=8)
+                in_ = half.rearrange("p j (q t i) -> p q t i j", t=4, i=8)
             else:
-                out = grouped[key][:].rearrange("p (t m j) -> p m j t", t=4, j=4)
-                in_ = raw[key][:].rearrange("p j (m t) -> p m j t", t=4)
+                out = grouped[key][:].rearrange("p (t e m j) -> p e t m j", t=4, m=2, j=4)
+                in_ = half.rearrange("p j (e m t) -> p e t m j", m=2, t=4)
             if eng == "V":
                 nc.vector.tensor_copy(out=out, in_=in_)
             else:
@@ -283,7 +289,7 @@ def tile_linearrecurrentunitcomplexeightstep_x1_kernel(tc, u, b, nu, theta, gamm
             return ("b", i // 2, i % 2, G)
 
         def cload(i):
-            load_c(ckeys[i][1], ckeys[i][2], ckeys[i][3])
+            load_c(ckeys[2 * i][1], ckeys[2 * i][2])
 
         def h_round(ch, G, engs="SS"):
             h_copy(engs[0], ch, G, 0)
@@ -309,8 +315,6 @@ def tile_linearrecurrentunitcomplexeightstep_x1_kernel(tc, u, b, nu, theta, gamm
         interleave("S", bk(0, 3))
         quant_w(bk(0, 2))
         load_u(3)
-        for i in range(4):
-            cload(i)
         interleave("V", bk(1, 0))
         quant_w(bk(0, 3))
         project(0, 0)
@@ -324,8 +328,8 @@ def tile_linearrecurrentunitcomplexeightstep_x1_kernel(tc, u, b, nu, theta, gamm
         u_transpose(1)
         quant_w(bk(1, 3))
         u_quant(1)
-        for i in range(4):
-            cload(4 + i)
+        cload(2)
+        cload(3)
         load_u(4)
         h_round(0, 0)
         project(0, 1)

@@ -26,6 +26,7 @@ def tile_linearrecurrentunitcomplexeightstep_x1_kernel(tc, u, b, nu, theta, gamm
         const = ctx.enter_context(tc.tile_pool(name="const", bufs=1))
         pool = ctx.enter_context(tc.tile_pool(name="work", bufs=1))
         psum = ctx.enter_context(tc.psum_pool(name="psum", bufs=1))
+        ctx.enter_context(tc.manual_schedule())
 
         v4 = const.tile([P, 1024], BF16, name="v4", align_bytes=64)
         v4p = const.tile([P, 1024], BF16, name="v4p", align_bytes=64)
@@ -64,23 +65,13 @@ def tile_linearrecurrentunitcomplexeightstep_x1_kernel(tc, u, b, nu, theta, gamm
 
         for i, vec in enumerate((nu, theta, gamma, d)):
             nc.scalar.dma_start(out=v4[i:i + 1, :], in_=vec.unsqueeze(0))
-        load_b(0, 0, 0)
-        load_b(0, 1, 0)
-        load_u(0)
-        load_b(1, 0, 0)
-        load_b(1, 1, 0)
-        for part in range(2):
-            for g in range(2):
-                load_b(part, g, 1)
-        load_u(1)
-        load_c(0, 0)
-        load_c(1, 0)
-        load_u(2)
 
         vecs = const.tile([P, 8, 4], F32, name="vecs")
         lam = const.tile([P, 6, 8], F32, name="lam")
 
-        def constants():
+        tmp = const.tile([P, 5, 8], F32, name="tmp")
+
+        def const_a():
             nc.vector.tensor_copy(
                 out=v4p[0:4, :].rearrange("p (G t q i) -> p G q t i", G=2, t=4, q=16),
                 in_=v4[0:4, :].rearrange("p (G q t i) -> p G q t i", G=2, t=4, q=16))
@@ -94,14 +85,17 @@ def tile_linearrecurrentunitcomplexeightstep_x1_kernel(tc, u, b, nu, theta, gamm
                 nc.tensor.transpose(dp[:, k, :], v4[:, 512 * g + t:512 * g + 512:4], ident16[:])
             nc.vector.tensor_copy(out=vecs[:, :, 3:4], in_=dp[:, :, 3:4])
 
-            tmp = const.tile([P, 5, 8], F32, name="tmp")
-            nc.scalar.activation(out=tmp[:, 0, :], in_=vecs[:, :, 0], func=ACT.Exp)
-            nc.scalar.activation(out=tmp[:, 1, :], in_=tmp[:, 0, :], func=ACT.Exp, scale=-1.0)
             nc.vector.tensor_scalar(out=tmp[:, 2, :], in0=vecs[:, :, 1], scalar1=-1.0, scalar2=math.pi / 2, op0=ALU.mult, op1=ALU.add)
-            nc.scalar.activation(out=tmp[:, 3, :], in_=vecs[:, :, 1], func=ACT.Sin)
-            nc.scalar.activation(out=tmp[:, 4, :], in_=tmp[:, 2, :], func=ACT.Sin)
             nc.vector.tensor_copy(out=lam[:, 3, :], in_=vecs[:, :, 2])
             nc.vector.tensor_copy(out=lam[:, 4, :], in_=vecs[:, :, 3])
+
+        def const_b():
+            nc.scalar.activation(out=tmp[:, 0, :], in_=vecs[:, :, 0], func=ACT.Exp)
+            nc.scalar.activation(out=tmp[:, 1, :], in_=tmp[:, 0, :], func=ACT.Exp, scale=-1.0)
+            nc.scalar.activation(out=tmp[:, 3, :], in_=vecs[:, :, 1], func=ACT.Sin)
+            nc.scalar.activation(out=tmp[:, 4, :], in_=tmp[:, 2, :], func=ACT.Sin)
+
+        def const_c():
             nc.vector.tensor_tensor(out=lam[:, 0, :], in0=tmp[:, 1, :], in1=tmp[:, 4, :], op=ALU.mult)
             nc.vector.tensor_tensor(out=lam[:, 1, :], in0=tmp[:, 1, :], in1=tmp[:, 3, :], op=ALU.mult)
             nc.vector.tensor_scalar(out=lam[:, 2, :], in0=lam[:, 1, :], scalar1=-1.0, scalar2=None, op0=ALU.mult)
@@ -181,27 +175,23 @@ def tile_linearrecurrentunitcomplexeightstep_x1_kernel(tc, u, b, nu, theta, gamm
                 state[ch, G] = pool.tile([P, 4, 2, w * P], F32, name="state", tag="state", bufs=4, align_bytes=64)
             nc.scalar.activation(out=state[ch, G][:, t, :, :], in_=acc[ch, n][:], func=ACT.Copy, scale=col(GAM, n))
 
-        def project(ch, G):
-            for t in range(4):
-                stage1(ch, 4 * G + t)
-                drain(ch, 4 * G + t)
+        def proj(ch, n):
+            stage1(ch, n)
+            drain(ch, n)
 
-        def recur(ch, G):
-            for s in range(len(CHUNKS[ch])):
-                if CHUNKS[ch][s] == 0:
-                    continue
-                if s > 0:
-                    prev = state[ch, G][:, :, :, P * (s - 1):P * s]
-                else:
-                    wp = len(CHUNKS[ch - 1])
-                    prev = state[ch - 1, G][:, :, :, P * (wp - 1):P * wp]
-                cur = state[ch, G][:, :, :, P * s:P * s + P]
-                for t in range(4):
-                    n = 4 * G + t
-                    nc.vector.scalar_tensor_tensor(out=cur[:, t, 0, :], in0=prev[:, t, 1, :], scalar=col(NLI, n), in1=cur[:, t, 0, :], op0=ALU.mult, op1=ALU.add)
-                    nc.vector.scalar_tensor_tensor(out=cur[:, t, 1, :], in0=prev[:, t, 0, :], scalar=col(LI, n), in1=cur[:, t, 1, :], op0=ALU.mult, op1=ALU.add)
-                for t in range(4):
-                    nc.vector.scalar_tensor_tensor(out=cur[:, t, :, :], in0=prev[:, t, :, :], scalar=col(LR, 4 * G + t), in1=cur[:, t, :, :], op0=ALU.mult, op1=ALU.add)
+        def rec(ch, G, s):
+            if s > 0:
+                prev = state[ch, G][:, :, :, P * (s - 1):P * s]
+            else:
+                wp = len(CHUNKS[ch - 1])
+                prev = state[ch - 1, G][:, :, :, P * (wp - 1):P * wp]
+            cur = state[ch, G][:, :, :, P * s:P * s + P]
+            for t in range(4):
+                n = 4 * G + t
+                nc.vector.scalar_tensor_tensor(out=cur[:, t, 0, :], in0=prev[:, t, 1, :], scalar=col(NLI, n), in1=cur[:, t, 0, :], op0=ALU.mult, op1=ALU.add)
+                nc.vector.scalar_tensor_tensor(out=cur[:, t, 1, :], in0=prev[:, t, 0, :], scalar=col(LI, n), in1=cur[:, t, 1, :], op0=ALU.mult, op1=ALU.add)
+            for t in range(4):
+                nc.vector.scalar_tensor_tensor(out=cur[:, t, :, :], in0=prev[:, t, :, :], scalar=col(LR, 4 * G + t), in1=cur[:, t, :, :], op0=ALU.mult, op1=ALU.add)
 
         hb = {}
         hq = {}
@@ -282,126 +272,273 @@ def tile_linearrecurrentunitcomplexeightstep_x1_kernel(tc, u, b, nu, theta, gamm
             if g == 1:
                 nc.sync.dma_start(out=out_0[:, t, :], in_=osb[ch, s][:])
 
-        n_ch = len(CHUNKS)
-        ckeys = [("c", part, G, g) for G in range(2) for part in range(2) for g in range(2)]
-
-        def bk(G, i):
-            return ("b", i // 2, i % 2, G)
-
-        def cload(i):
-            load_c(ckeys[2 * i][1], ckeys[2 * i][2])
-
-        def h_round(ch, G, engs="SS"):
-            h_copy(engs[0], ch, G, 0)
-            h_copy(engs[1], ch, G, 1)
-
-        def back(ch, g):
-            for j in range(4):
-                skip_add(ch, 4 * g + j)
-
-        def out(ch, g, engs="SSS"):
-            y_round(engs[0], ch, g)
-            for s in range(len(CHUNKS[ch])):
-                y_store(engs[1 + s], ch, g, s)
-
-        interleave("V", bk(0, 0))
-        interleave("S", bk(0, 1))
-        constants()
-        quant_w(bk(0, 0))
-        u_transpose(0)
-        interleave("V", bk(0, 2))
-        u_quant(0)
-        quant_w(bk(0, 1))
-        interleave("S", bk(0, 3))
-        quant_w(bk(0, 2))
-        load_u(3)
-        interleave("V", bk(1, 0))
-        quant_w(bk(0, 3))
-        project(0, 0)
-        quant_w(bk(1, 0))
-        interleave("V", bk(1, 1))
-        interleave("S", bk(1, 2))
-        recur(0, 0)
-        quant_w(bk(1, 1))
-        interleave("V", bk(1, 3))
-        quant_w(bk(1, 2))
-        u_transpose(1)
-        quant_w(bk(1, 3))
-        u_quant(1)
-        cload(2)
-        cload(3)
-        load_u(4)
-        h_round(0, 0)
-        project(0, 1)
-        project(1, 0)
-        interleave("V", ckeys[0])
-        recur(0, 1)
-        quant_w(ckeys[0])
-        h_quant(0, 0)
-        interleave("S", ckeys[1])
-        interleave("V", ckeys[2])
-        recur(1, 0)
-        quant_w(ckeys[2])
-        h_round(0, 1)
-        project(1, 1)
-        u_transpose(2)
-        quant_w(ckeys[1])
-        interleave("V", ckeys[3])
-        u_quant(2)
-        quant_w(ckeys[3])
-        h_round(1, 0)
-        interleave("V", ckeys[4])
-        recur(1, 1)
-        quant_w(ckeys[4])
-        h_quant(0, 1)
-        interleave("S", ckeys[5])
-        h_quant(1, 0)
-        interleave("V", ckeys[6])
-        project(2, 0)
-        quant_w(ckeys[5])
-        quant_w(ckeys[6])
-        interleave("V", ckeys[7])
-        recur(2, 0)
-        quant_w(ckeys[7])
-        for k in range(8):
-            stage2(0, k)
-        h_round(1, 1)
-        back(0, 0)
-        back(0, 1)
-        for k in range(2, n_ch):
-            project(k, 1)
-            h_round(k, 0)
-            h_quant(k - 1, 1)
-            out(k - 2, 0)
-            for j in range(8):
-                stage2(k - 1, j)
-            recur(k, 1)
-            if k + 1 < n_ch:
-                u_transpose(k + 1)
-                u_quant(k + 1)
-                project(k + 1, 0)
-            h_quant(k, 0)
-            out(k - 2, 1)
-            back(k - 1, 0)
-            back(k - 1, 1)
-            h_round(k, 1)
-            if k + 1 < n_ch:
-                recur(k + 1, 0)
-        h_quant(n_ch - 1, 1)
-        out(n_ch - 2, 0)
-        for j in range(8):
-            stage2(n_ch - 1, j)
-        out(n_ch - 2, 1)
-        back(n_ch - 1, 0)
-        out(n_ch - 1, 0)
-        back(n_ch - 1, 1)
-        out(n_ch - 1, 1)
-
         ysc = const.tile([P, 2, 1024], U8, name="ysc", align_bytes=64)
-        for g in range(2):
-            yq = const.tile([P, 1024], U32, name="yq%d" % g, align_bytes=64)
-            nc.vector.quantize_mx(out=yq[:].bitcast(FP8X4), scales=ysc[:, g, :], in_=yb[g][:].rearrange("p n s t -> p (n s t)"))
-            nc.sync.dma_start(out=out_1[g].rearrange("p m t -> p (m t)").bitcast(I32), in_=yq[:].bitcast(I32))
+        yq = {}
+
+        def plane(g, h):
+            yq[g, h] = const.tile([P, 512], U32, name="yq%d%d" % (g, h), align_bytes=64)
+            nc.vector.quantize_mx(
+                out=yq[g, h][:].bitcast(FP8X4), scales=ysc[:, g, 512 * h:512 * h + 512],
+                in_=yb[g][:, 64 * h:64 * h + 64, :, :].rearrange("p n s t -> p (n s t)"))
+            nc.sync.dma_start(out=out_1[g, :, 512 * h:512 * h + 512, :].rearrange("p m t -> p (m t)").bitcast(I32), in_=yq[g, h][:].bitcast(I32))
+
+        load_b(0, 0, 0)
+        const_a()
+        load_b(1, 1, 1)
+        interleave("V", ("b", 1, 1, 1))
+        interleave("S", ("b", 0, 0, 0))
+        load_b(1, 0, 0)
+        interleave("V", ("b", 1, 0, 0))
+        load_u(0)
+        load_b(1, 1, 0)
+        quant_w(("b", 0, 0, 0))
+        load_b(0, 1, 0)
+        load_u(1)
+        quant_w(("b", 1, 1, 1))
+        const_b()
+        const_c()
+        u_transpose(0)
+        u_quant(0)
+        interleave("V", ("b", 0, 1, 0))
+        load_b(0, 0, 1)
+        quant_w(("b", 1, 0, 0))
+        interleave("S", ("b", 1, 1, 0))
+        load_b(0, 1, 1)
+        quant_w(("b", 1, 1, 0))
+        quant_w(("b", 0, 1, 0))
+        load_b(1, 0, 1)
+        u_transpose(1)
+        interleave("S", ("b", 0, 0, 1))
+        u_quant(1)
+        proj(0, 2)
+        proj(1, 1)
+        interleave("V", ("b", 0, 1, 1))
+        proj(0, 0)
+        interleave("V", ("b", 1, 0, 1))
+        quant_w(("b", 0, 0, 1))
+        load_c(0, 0)
+        proj(0, 1)
+        proj(0, 3)
+        quant_w(("b", 1, 0, 1))
+        load_c(1, 0)
+        proj(1, 0)
+        quant_w(("b", 0, 1, 1))
+        proj(1, 3)
+        interleave("V", ("c", 0, 0, 0))
+        rec(0, 0, 1)
+        proj(0, 7)
+        quant_w(("c", 0, 0, 0))
+        proj(0, 4)
+        load_u(2)
+        proj(1, 4)
+        proj(1, 2)
+        proj(0, 6)
+        h_copy("S", 0, 0, 1)
+        interleave("V", ("c", 1, 0, 0))
+        load_u(4)
+        interleave("V", ("c", 0, 0, 1))
+        u_transpose(2)
+        quant_w(("c", 1, 0, 0))
+        proj(1, 5)
+        h_copy("S", 0, 0, 0)
+        load_u(3)
+        rec(1, 0, 0)
+        proj(0, 5)
+        u_quant(2)
+        interleave("S", ("c", 1, 0, 1))
+        rec(0, 1, 1)
+        proj(2, 0)
+        load_c(1, 1)
+        proj(2, 1)
+        load_c(0, 1)
+        proj(2, 3)
+        proj(1, 6)
+        proj(2, 2)
+        u_transpose(3)
+        rec(1, 0, 1)
+        rec(2, 0, 0)
+        h_copy("S", 0, 1, 1)
+        quant_w(("c", 1, 0, 1))
+        proj(1, 7)
+        h_copy("S", 1, 0, 1)
+        quant_w(("c", 0, 0, 1))
+        interleave("S", ("c", 0, 1, 0))
+        h_copy("V", 1, 0, 0)
+        h_copy("S", 0, 1, 0)
+        proj(2, 7)
+        rec(1, 1, 0)
+        interleave("S", ("c", 1, 1, 0))
+        proj(2, 6)
+        rec(1, 1, 1)
+        proj(2, 4)
+        h_quant(0, 0)
+        interleave("S", ("c", 0, 1, 1))
+        quant_w(("c", 0, 1, 0))
+        proj(2, 5)
+        h_quant(0, 1)
+        interleave("S", ("c", 1, 1, 1))
+        u_quant(3)
+        rec(2, 0, 1)
+        proj(3, 2)
+        u_transpose(4)
+        proj(3, 0)
+        quant_w(("c", 1, 1, 0))
+        quant_w(("c", 0, 1, 1))
+        rec(2, 1, 0)
+        quant_w(("c", 1, 1, 1))
+        proj(3, 1)
+        stage2(0, 0)
+        skip_add(0, 0)
+        h_copy("S", 2, 0, 1)
+        stage2(0, 1)
+        h_copy("S", 1, 1, 0)
+        proj(3, 3)
+        stage2(0, 2)
+        h_copy("S", 1, 1, 1)
+        stage2(0, 3)
+        skip_add(0, 1)
+        skip_add(0, 2)
+        stage2(0, 4)
+        skip_add(0, 3)
+        rec(2, 1, 1)
+        stage2(0, 6)
+        h_copy("S", 2, 0, 0)
+        proj(3, 4)
+        stage2(0, 5)
+        proj(3, 6)
+        y_store("S", 0, 0, 0)
+        proj(3, 5)
+        h_quant(1, 0)
+        skip_add(0, 6)
+        skip_add(0, 4)
+        y_store("S", 0, 0, 1)
+        skip_add(0, 5)
+        stage2(0, 7)
+        u_quant(4)
+        h_copy("S", 2, 1, 1)
+        h_quant(1, 1)
+        proj(3, 7)
+        stage2(1, 0)
+        rec(3, 0, 0)
+        proj(4, 7)
+        stage2(1, 6)
+        skip_add(0, 7)
+        stage2(1, 7)
+        h_quant(2, 0)
+        proj(4, 4)
+        stage2(1, 1)
+        skip_add(1, 1)
+        h_copy("S", 2, 1, 0)
+        skip_add(1, 7)
+        skip_add(1, 6)
+        stage2(1, 2)
+        proj(4, 6)
+        skip_add(1, 0)
+        rec(3, 1, 0)
+        proj(4, 5)
+        h_quant(2, 1)
+        h_copy("S", 3, 0, 1)
+        stage2(1, 3)
+        y_store("S", 0, 1, 0)
+        proj(4, 0)
+        skip_add(1, 2)
+        stage2(1, 4)
+        y_round("S", 0, 0)
+        stage2(1, 5)
+        skip_add(1, 5)
+        skip_add(1, 3)
+        y_store("S", 0, 1, 1)
+        stage2(2, 2)
+        skip_add(1, 4)
+        y_round("S", 1, 0)
+        h_copy("S", 3, 1, 1)
+        proj(4, 1)
+        rec(4, 1, 0)
+        h_copy("S", 3, 1, 0)
+        skip_add(2, 2)
+        stage2(2, 3)
+        stage2(2, 6)
+        y_round("V", 0, 1)
+        h_copy("S", 3, 0, 0)
+        stage2(2, 0)
+        skip_add(2, 0)
+        y_store("S", 1, 0, 0)
+        y_store("S", 1, 1, 0)
+        skip_add(2, 3)
+        stage2(2, 7)
+        skip_add(2, 7)
+        stage2(2, 1)
+        proj(4, 2)
+        skip_add(2, 6)
+        proj(4, 3)
+        stage2(2, 4)
+        h_quant(3, 1)
+        y_store("S", 1, 0, 1)
+        stage2(2, 5)
+        h_quant(3, 0)
+        skip_add(2, 4)
+        skip_add(2, 1)
+        rec(4, 0, 0)
+        stage2(3, 0)
+        stage2(3, 4)
+        h_copy("S", 4, 1, 0)
+        skip_add(2, 5)
+        stage2(3, 2)
+        h_copy("V", 4, 0, 1)
+        h_copy("S", 4, 1, 1)
+        y_store("S", 2, 0, 0)
+        y_store("S", 1, 1, 1)
+        h_copy("V", 4, 0, 0)
+        skip_add(3, 2)
+        stage2(3, 3)
+        stage2(3, 6)
+        y_store("V", 2, 1, 0)
+        stage2(3, 1)
+        y_round("S", 1, 1)
+        h_quant(4, 0)
+        y_round("S", 2, 0)
+        h_quant(4, 1)
+        y_store("S", 2, 0, 1)
+        skip_add(3, 0)
+        y_store("V", 2, 1, 1)
+        skip_add(3, 1)
+        stage2(4, 0)
+        skip_add(3, 3)
+        stage2(4, 3)
+        stage2(4, 1)
+        stage2(4, 2)
+        y_round("S", 3, 0)
+        stage2(3, 5)
+        skip_add(4, 0)
+        skip_add(4, 3)
+        skip_add(3, 4)
+        stage2(4, 4)
+        skip_add(4, 1)
+        y_round("S", 2, 1)
+        skip_add(4, 2)
+        skip_add(3, 5)
+        skip_add(3, 6)
+        stage2(3, 7)
+        stage2(4, 6)
+        y_round("V", 4, 0)
+        skip_add(3, 7)
+        plane(0, 1)
+        plane(0, 0)
+        y_store("S", 3, 0, 0)
+        y_store("S", 3, 1, 0)
+        skip_add(4, 6)
+        skip_add(4, 4)
+        stage2(4, 7)
+        y_round("S", 3, 1)
+        stage2(4, 5)
+        skip_add(4, 5)
+        skip_add(4, 7)
+        y_store("V", 4, 0, 0)
+        y_store("S", 4, 1, 0)
+        y_round("V", 4, 1)
+        plane(1, 1)
+        plane(1, 0)
+
         for q in range(4):
             nc.sync.dma_start(
                 out=out_2[:, 4 * q:4 * q + 4, :].bitcast(I32).rearrange("g r m -> r g m"),

@@ -26,7 +26,6 @@ def tile_linearrecurrentunitcomplexeightstep_x1_kernel(tc, u, b, nu, theta, gamm
         const = ctx.enter_context(tc.tile_pool(name="const", bufs=1))
         pool = ctx.enter_context(tc.tile_pool(name="work", bufs=1))
         psum = ctx.enter_context(tc.psum_pool(name="psum", bufs=1))
-        ctx.enter_context(tc.manual_schedule())
 
         v4 = const.tile([P, 1024], BF16, name="v4", align_bytes=64)
         v4p = const.tile([P, 1024], BF16, name="v4p", align_bytes=64)
@@ -67,7 +66,7 @@ def tile_linearrecurrentunitcomplexeightstep_x1_kernel(tc, u, b, nu, theta, gamm
             nc.scalar.dma_start(out=v4[i:i + 1, :], in_=vec.unsqueeze(0))
 
         vecs = const.tile([P, 8, 4], F32, name="vecs")
-        lam = const.tile([P, 6, 8], F32, name="lam")
+        lam = const.tile([P, 3, 8], F32, name="lam")
 
         tmp = const.tile([P, 5, 8], F32, name="tmp")
 
@@ -86,8 +85,6 @@ def tile_linearrecurrentunitcomplexeightstep_x1_kernel(tc, u, b, nu, theta, gamm
             nc.vector.tensor_copy(out=vecs[:, :, 3:4], in_=dp[:, :, 3:4])
 
             nc.vector.tensor_scalar(out=tmp[:, 2, :], in0=vecs[:, :, 1], scalar1=-1.0, scalar2=math.pi / 2, op0=ALU.mult, op1=ALU.add)
-            nc.vector.tensor_copy(out=lam[:, 3, :], in_=vecs[:, :, 2])
-            nc.vector.tensor_copy(out=lam[:, 4, :], in_=vecs[:, :, 3])
 
         def const_b():
             nc.scalar.activation(out=tmp[:, 0, :], in_=vecs[:, :, 0], func=ACT.Exp)
@@ -100,7 +97,7 @@ def tile_linearrecurrentunitcomplexeightstep_x1_kernel(tc, u, b, nu, theta, gamm
             nc.vector.tensor_tensor(out=lam[:, 1, :], in0=tmp[:, 1, :], in1=tmp[:, 3, :], op=ALU.mult)
             nc.vector.tensor_scalar(out=lam[:, 2, :], in0=lam[:, 1, :], scalar1=-1.0, scalar2=None, op0=ALU.mult)
 
-        LR, LI, NLI, GAM, DD = range(5)
+        LR, LI, NLI = range(3)
 
         def col(which, k):
             return lam[:, which, k:k + 1]
@@ -173,7 +170,7 @@ def tile_linearrecurrentunitcomplexeightstep_x1_kernel(tc, u, b, nu, theta, gamm
             G, t = divmod(n, 4)
             if (ch, G) not in state:
                 state[ch, G] = pool.tile([P, 4, 2, w * P], F32, name="state", tag="state", bufs=4, align_bytes=64)
-            nc.scalar.activation(out=state[ch, G][:, t, :, :], in_=acc[ch, n][:], func=ACT.Copy, scale=col(GAM, n))
+            nc.scalar.activation(out=state[ch, G][:, t, :, :], in_=acc[ch, n][:], func=ACT.Copy, scale=vecs[:, n, 2:3])
 
         def proj(ch, n):
             stage1(ch, n)
@@ -241,7 +238,7 @@ def tile_linearrecurrentunitcomplexeightstep_x1_kernel(tc, u, b, nu, theta, gamm
             if (ch, g) not in ysb:
                 ysb[ch, g] = pool.tile([P, 4, w * P], F32, name="ysb", tag="ysb", bufs=4, align_bytes=64)
             nc.vector.scalar_tensor_tensor(
-                out=ysb[ch, g][:, t, :], in0=ug[ch][:, g, :, t], scalar=col(DD, k), in1=yp[ch, k // per][:, k % per, :], op0=ALU.mult, op1=ALU.add)
+                out=ysb[ch, g][:, t, :], in0=ug[ch][:, g, :, t], scalar=vecs[:, k, 3:4], in1=yp[ch, k // per][:, k % per, :], op0=ALU.mult, op1=ALU.add)
 
         def y_round(eng, ch, g):
             w = len(CHUNKS[ch])
@@ -283,261 +280,261 @@ def tile_linearrecurrentunitcomplexeightstep_x1_kernel(tc, u, b, nu, theta, gamm
             nc.sync.dma_start(out=out_1[g, :, 512 * h:512 * h + 512, :].rearrange("p m t -> p (m t)").bitcast(I32), in_=yq[g, h][:].bitcast(I32))
 
         load_b(0, 0, 0)
-        const_a()
-        load_b(1, 1, 1)
-        interleave("V", ("b", 1, 1, 1))
-        interleave("S", ("b", 0, 0, 0))
-        load_b(1, 0, 0)
-        interleave("V", ("b", 1, 0, 0))
-        load_u(0)
-        load_b(1, 1, 0)
-        quant_w(("b", 0, 0, 0))
         load_b(0, 1, 0)
-        load_u(1)
-        quant_w(("b", 1, 1, 1))
+        load_u(0)
+        load_b(1, 0, 0)
+        load_b(1, 1, 0)
+        load_b(0, 0, 1)
+        interleave("V", ("b", 0, 0, 0))
+        load_b(0, 1, 1)
+        interleave("S", ("b", 0, 1, 0))
+        load_b(1, 0, 1)
+        const_a()
         const_b()
         const_c()
+        quant_w(("b", 0, 0, 0))
         u_transpose(0)
-        u_quant(0)
-        interleave("V", ("b", 0, 1, 0))
-        load_b(0, 0, 1)
-        quant_w(("b", 1, 0, 0))
-        interleave("S", ("b", 1, 1, 0))
-        load_b(0, 1, 1)
-        quant_w(("b", 1, 1, 0))
-        quant_w(("b", 0, 1, 0))
-        load_b(1, 0, 1)
-        u_transpose(1)
-        interleave("S", ("b", 0, 0, 1))
-        u_quant(1)
-        proj(0, 2)
-        proj(1, 1)
-        interleave("V", ("b", 0, 1, 1))
-        proj(0, 0)
-        interleave("V", ("b", 1, 0, 1))
-        quant_w(("b", 0, 0, 1))
+        interleave("V", ("b", 1, 0, 0))
+        load_b(1, 1, 1)
+        load_u(1)
         load_c(0, 0)
-        proj(0, 1)
-        proj(0, 3)
-        quant_w(("b", 1, 0, 1))
         load_c(1, 0)
-        proj(1, 0)
+        u_quant(0)
+        quant_w(("b", 0, 1, 0))
+        interleave("S", ("b", 1, 1, 0))
+        quant_w(("b", 1, 0, 0))
+        load_u(2)
+        interleave("V", ("b", 0, 0, 1))
+        quant_w(("b", 1, 1, 0))
+        proj(0, 0)
+        proj(0, 1)
+        proj(0, 2)
+        proj(0, 3)
+        quant_w(("b", 0, 0, 1))
+        interleave("V", ("b", 0, 1, 1))
+        interleave("S", ("b", 1, 0, 1))
+        rec(0, 0, 1)
         quant_w(("b", 0, 1, 1))
+        interleave("V", ("b", 1, 1, 1))
+        quant_w(("b", 1, 0, 1))
+        u_transpose(1)
+        load_u(3)
+        quant_w(("b", 1, 1, 1))
+        u_quant(1)
+        h_copy("S", 0, 0, 0)
+        h_copy("S", 0, 0, 1)
+        proj(0, 4)
+        proj(0, 5)
+        proj(0, 6)
+        proj(0, 7)
+        proj(1, 0)
+        proj(1, 1)
+        proj(1, 2)
         proj(1, 3)
         interleave("V", ("c", 0, 0, 0))
-        rec(0, 0, 1)
-        proj(0, 7)
-        quant_w(("c", 0, 0, 0))
-        proj(0, 4)
-        load_u(2)
-        proj(1, 4)
-        proj(1, 2)
-        proj(0, 6)
-        h_copy("S", 0, 0, 1)
-        interleave("V", ("c", 1, 0, 0))
-        load_u(4)
-        interleave("V", ("c", 0, 0, 1))
-        u_transpose(2)
-        quant_w(("c", 1, 0, 0))
-        proj(1, 5)
-        h_copy("S", 0, 0, 0)
-        load_u(3)
-        rec(1, 0, 0)
-        proj(0, 5)
-        u_quant(2)
-        interleave("S", ("c", 1, 0, 1))
         rec(0, 1, 1)
-        proj(2, 0)
-        load_c(1, 1)
-        proj(2, 1)
-        load_c(0, 1)
-        proj(2, 3)
-        proj(1, 6)
-        proj(2, 2)
-        u_transpose(3)
-        rec(1, 0, 1)
-        rec(2, 0, 0)
-        h_copy("S", 0, 1, 1)
-        quant_w(("c", 1, 0, 1))
-        proj(1, 7)
-        h_copy("S", 1, 0, 1)
-        quant_w(("c", 0, 0, 1))
-        interleave("S", ("c", 0, 1, 0))
-        h_copy("V", 1, 0, 0)
-        h_copy("S", 0, 1, 0)
-        proj(2, 7)
-        rec(1, 1, 0)
-        interleave("S", ("c", 1, 1, 0))
-        proj(2, 6)
-        rec(1, 1, 1)
-        proj(2, 4)
+        quant_w(("c", 0, 0, 0))
         h_quant(0, 0)
-        interleave("S", ("c", 0, 1, 1))
+        interleave("S", ("c", 0, 0, 1))
+        load_c(0, 1)
+        interleave("V", ("c", 1, 0, 0))
+        rec(1, 0, 0)
+        rec(1, 0, 1)
+        quant_w(("c", 1, 0, 0))
+        h_copy("S", 0, 1, 0)
+        h_copy("S", 0, 1, 1)
+        proj(1, 4)
+        proj(1, 5)
+        proj(1, 6)
+        proj(1, 7)
+        u_transpose(2)
+        load_u(4)
+        quant_w(("c", 0, 0, 1))
+        interleave("S", ("c", 1, 0, 1))
+        load_c(1, 1)
+        u_quant(2)
+        quant_w(("c", 1, 0, 1))
+        h_copy("S", 1, 0, 0)
+        h_copy("S", 1, 0, 1)
+        interleave("V", ("c", 0, 1, 0))
+        rec(1, 1, 0)
+        rec(1, 1, 1)
         quant_w(("c", 0, 1, 0))
-        proj(2, 5)
         h_quant(0, 1)
-        interleave("S", ("c", 1, 1, 1))
-        u_quant(3)
-        rec(2, 0, 1)
-        proj(3, 2)
-        u_transpose(4)
-        proj(3, 0)
-        quant_w(("c", 1, 1, 0))
+        interleave("S", ("c", 0, 1, 1))
+        h_quant(1, 0)
+        interleave("V", ("c", 1, 1, 0))
+        proj(2, 0)
+        proj(2, 1)
+        proj(2, 2)
+        proj(2, 3)
         quant_w(("c", 0, 1, 1))
-        rec(2, 1, 0)
+        quant_w(("c", 1, 1, 0))
+        interleave("S", ("c", 1, 1, 1))
+        rec(2, 0, 0)
+        rec(2, 0, 1)
         quant_w(("c", 1, 1, 1))
-        proj(3, 1)
         stage2(0, 0)
-        skip_add(0, 0)
-        h_copy("S", 2, 0, 1)
         stage2(0, 1)
-        h_copy("S", 1, 1, 0)
-        proj(3, 3)
         stage2(0, 2)
-        h_copy("S", 1, 1, 1)
         stage2(0, 3)
+        h_copy("S", 1, 1, 0)
+        h_copy("S", 1, 1, 1)
+        skip_add(0, 0)
         skip_add(0, 1)
         skip_add(0, 2)
-        stage2(0, 4)
         skip_add(0, 3)
-        rec(2, 1, 1)
-        stage2(0, 6)
-        h_copy("S", 2, 0, 0)
-        proj(3, 4)
+        stage2(0, 4)
         stage2(0, 5)
-        proj(3, 6)
-        y_store("S", 0, 0, 0)
-        proj(3, 5)
-        h_quant(1, 0)
-        skip_add(0, 6)
-        skip_add(0, 4)
-        y_store("S", 0, 0, 1)
-        skip_add(0, 5)
+        stage2(0, 6)
         stage2(0, 7)
-        u_quant(4)
-        h_copy("S", 2, 1, 1)
-        h_quant(1, 1)
-        proj(3, 7)
-        stage2(1, 0)
-        rec(3, 0, 0)
-        proj(4, 7)
-        stage2(1, 6)
+        skip_add(0, 4)
+        skip_add(0, 5)
+        skip_add(0, 6)
         skip_add(0, 7)
+        proj(2, 4)
+        proj(2, 5)
+        proj(2, 6)
+        proj(2, 7)
+        h_copy("S", 2, 0, 0)
+        h_copy("S", 2, 0, 1)
+        h_quant(1, 1)
+        y_round("S", 0, 0)
+        y_store("S", 0, 0, 0)
+        y_store("S", 0, 0, 1)
+        stage2(1, 0)
+        stage2(1, 1)
+        stage2(1, 2)
+        stage2(1, 3)
+        rec(2, 1, 0)
+        rec(2, 1, 1)
+        u_transpose(3)
+        u_quant(3)
+        proj(3, 0)
+        proj(3, 1)
+        proj(3, 2)
+        proj(3, 3)
+        skip_add(1, 0)
+        skip_add(1, 1)
+        skip_add(1, 2)
+        skip_add(1, 3)
+        stage2(1, 4)
+        stage2(1, 5)
+        stage2(1, 6)
         stage2(1, 7)
         h_quant(2, 0)
-        proj(4, 4)
-        stage2(1, 1)
-        skip_add(1, 1)
-        h_copy("S", 2, 1, 0)
-        skip_add(1, 7)
-        skip_add(1, 6)
-        stage2(1, 2)
-        proj(4, 6)
-        skip_add(1, 0)
-        rec(3, 1, 0)
-        proj(4, 5)
-        h_quant(2, 1)
-        h_copy("S", 3, 0, 1)
-        stage2(1, 3)
+        y_round("S", 0, 1)
         y_store("S", 0, 1, 0)
-        proj(4, 0)
-        skip_add(1, 2)
-        stage2(1, 4)
-        y_round("S", 0, 0)
-        stage2(1, 5)
-        skip_add(1, 5)
-        skip_add(1, 3)
         y_store("S", 0, 1, 1)
-        stage2(2, 2)
         skip_add(1, 4)
-        y_round("S", 1, 0)
-        h_copy("S", 3, 1, 1)
-        proj(4, 1)
-        rec(4, 1, 0)
-        h_copy("S", 3, 1, 0)
-        skip_add(2, 2)
-        stage2(2, 3)
-        stage2(2, 6)
-        y_round("V", 0, 1)
+        skip_add(1, 5)
+        skip_add(1, 6)
+        skip_add(1, 7)
+        h_copy("S", 2, 1, 0)
+        h_copy("S", 2, 1, 1)
+        rec(3, 0, 0)
+        proj(3, 4)
+        proj(3, 5)
+        proj(3, 6)
+        proj(3, 7)
         h_copy("S", 3, 0, 0)
-        stage2(2, 0)
-        skip_add(2, 0)
+        h_copy("S", 3, 0, 1)
+        h_quant(2, 1)
+        y_round("S", 1, 0)
         y_store("S", 1, 0, 0)
-        y_store("S", 1, 1, 0)
-        skip_add(2, 3)
-        stage2(2, 7)
-        skip_add(2, 7)
-        stage2(2, 1)
-        proj(4, 2)
-        skip_add(2, 6)
-        proj(4, 3)
-        stage2(2, 4)
-        h_quant(3, 1)
         y_store("S", 1, 0, 1)
-        stage2(2, 5)
-        h_quant(3, 0)
-        skip_add(2, 4)
+        stage2(2, 0)
+        stage2(2, 1)
+        stage2(2, 2)
+        stage2(2, 3)
+        rec(3, 1, 0)
+        u_transpose(4)
+        u_quant(4)
+        proj(4, 0)
+        proj(4, 1)
+        proj(4, 2)
+        proj(4, 3)
+        skip_add(2, 0)
         skip_add(2, 1)
-        rec(4, 0, 0)
-        stage2(3, 0)
-        stage2(3, 4)
-        h_copy("S", 4, 1, 0)
-        skip_add(2, 5)
-        stage2(3, 2)
-        h_copy("V", 4, 0, 1)
-        h_copy("S", 4, 1, 1)
-        y_store("S", 2, 0, 0)
-        y_store("S", 1, 1, 1)
-        h_copy("V", 4, 0, 0)
-        skip_add(3, 2)
-        stage2(3, 3)
-        stage2(3, 6)
-        y_store("V", 2, 1, 0)
-        stage2(3, 1)
+        skip_add(2, 2)
+        skip_add(2, 3)
+        stage2(2, 4)
+        stage2(2, 5)
+        stage2(2, 6)
+        stage2(2, 7)
+        h_quant(3, 0)
         y_round("S", 1, 1)
-        h_quant(4, 0)
+        y_store("S", 1, 1, 0)
+        y_store("S", 1, 1, 1)
+        skip_add(2, 4)
+        skip_add(2, 5)
+        skip_add(2, 6)
+        skip_add(2, 7)
+        h_copy("S", 3, 1, 0)
+        h_copy("S", 3, 1, 1)
+        rec(4, 0, 0)
+        proj(4, 4)
+        proj(4, 5)
+        proj(4, 6)
+        proj(4, 7)
+        h_copy("S", 4, 0, 0)
+        h_copy("S", 4, 0, 1)
+        h_quant(3, 1)
         y_round("S", 2, 0)
-        h_quant(4, 1)
+        y_store("S", 2, 0, 0)
         y_store("S", 2, 0, 1)
+        stage2(3, 0)
+        stage2(3, 1)
+        stage2(3, 2)
+        stage2(3, 3)
+        rec(4, 1, 0)
         skip_add(3, 0)
-        y_store("V", 2, 1, 1)
         skip_add(3, 1)
-        stage2(4, 0)
+        skip_add(3, 2)
         skip_add(3, 3)
-        stage2(4, 3)
-        stage2(4, 1)
-        stage2(4, 2)
-        y_round("S", 3, 0)
+        stage2(3, 4)
         stage2(3, 5)
-        skip_add(4, 0)
-        skip_add(4, 3)
-        skip_add(3, 4)
-        stage2(4, 4)
-        skip_add(4, 1)
+        stage2(3, 6)
+        stage2(3, 7)
+        h_quant(4, 0)
         y_round("S", 2, 1)
-        skip_add(4, 2)
+        y_store("S", 2, 1, 0)
+        y_store("S", 2, 1, 1)
+        skip_add(3, 4)
         skip_add(3, 5)
         skip_add(3, 6)
-        stage2(3, 7)
-        stage2(4, 6)
-        y_round("V", 4, 0)
         skip_add(3, 7)
-        plane(0, 1)
-        plane(0, 0)
+        h_copy("S", 4, 1, 0)
+        h_copy("S", 4, 1, 1)
+        h_quant(4, 1)
+        y_round("S", 3, 0)
         y_store("S", 3, 0, 0)
-        y_store("S", 3, 1, 0)
-        skip_add(4, 6)
-        skip_add(4, 4)
-        stage2(4, 7)
+        stage2(4, 0)
+        stage2(4, 1)
+        stage2(4, 2)
+        stage2(4, 3)
         y_round("S", 3, 1)
+        y_store("S", 3, 1, 0)
+        skip_add(4, 0)
+        skip_add(4, 1)
+        skip_add(4, 2)
+        skip_add(4, 3)
+        stage2(4, 4)
         stage2(4, 5)
+        stage2(4, 6)
+        stage2(4, 7)
+        y_round("S", 4, 0)
+        y_store("S", 4, 0, 0)
+        skip_add(4, 4)
         skip_add(4, 5)
+        skip_add(4, 6)
         skip_add(4, 7)
-        y_store("V", 4, 0, 0)
+        y_round("S", 4, 1)
         y_store("S", 4, 1, 0)
-        y_round("V", 4, 1)
-        plane(1, 1)
+        plane(0, 0)
+        plane(0, 1)
         plane(1, 0)
+        plane(1, 1)
 
         for q in range(4):
             nc.sync.dma_start(

@@ -29,10 +29,12 @@ def tile_linearrecurrentunitcomplexeightstep_x1_kernel(tc, u, b, nu, theta, gamm
 
         v4 = const.tile([P, 1024], BF16, name="v4", align_bytes=64)
         v4p = const.tile([P, 1024], BF16, name="v4p", align_bytes=64)
+        nc.vector.memset(v4[:], 0.0)
+        for i, vec in enumerate((nu, theta, gamma, d)):
+            nc.scalar.dma_start(out=v4[i:i + 1, :], in_=vec.unsqueeze(0))
         warm = const.tile([P, 2], F32, name="warm")
         nc.vector.memset(warm[:], 0.0)
         nc.scalar.activation(out=warm[:, 1:2], in_=warm[:, 0:1], func=ACT.Exp)
-        nc.vector.memset(v4[:], 0.0)
         nc.gpsimd.memset(v4p[:], 0.0)
         ident32 = const.tile([P, P], F32, name="ident32")
         make_identity(nc, ident32[:])
@@ -49,11 +51,13 @@ def tile_linearrecurrentunitcomplexeightstep_x1_kernel(tc, u, b, nu, theta, gamm
 
         raw = {}
 
-        def load_b(part, g, G):
+        def load_b(part, g, G, pieces=1):
             raw["b", part, g, G] = pool.tile([P, 4, 512], BF16, name="raw_b", tag="raw_b", bufs=5, align_bytes=64)
-            nc.sync.dma_start(
-                out=raw["b", part, g, G][:],
-                in_=b[part, 512 * g:512 * g + 512, 512 * G:512 * G + 512].rearrange("(p j) w -> p j w", j=4))
+            step = 512 // pieces
+            for lo in range(0, 512, step):
+                nc.sync.dma_start(
+                    out=raw["b", part, g, G][:, :, lo:lo + step],
+                    in_=b[part, 512 * g:512 * g + 512, 512 * G + lo:512 * G + lo + step].rearrange("(p j) w -> p j w", j=4))
 
         def load_c(part, G):
             raw["c", part, G] = pool.tile([P, 4, 1024], BF16, name="raw_c", tag="raw_c", bufs=2, align_bytes=64)
@@ -62,8 +66,6 @@ def tile_linearrecurrentunitcomplexeightstep_x1_kernel(tc, u, b, nu, theta, gamm
                     out=raw["c", part, G][:, j, :],
                     in_=c[part, 512 * G:512 * G + 512, :].rearrange("(q j i) w -> j q i w", j=4, i=8)[j])
 
-        for i, vec in enumerate((nu, theta, gamma, d)):
-            nc.scalar.dma_start(out=v4[i:i + 1, :], in_=vec.unsqueeze(0))
 
         vecs = const.tile([P, 8, 4], F32, name="vecs")
         lam = const.tile([P, 3, 8], F32, name="lam")
@@ -106,7 +108,7 @@ def tile_linearrecurrentunitcomplexeightstep_x1_kernel(tc, u, b, nu, theta, gamm
         codes = {}
         scales = {}
 
-        def interleave(eng, key):
+        def interleave(eng, key, pieces=1):
             grouped[key] = pool.tile([P, 2048], BF16, name="grouped", tag="grouped", bufs=3, align_bytes=64)
             half = raw[key][:] if key[0] == "b" else raw[key[:3]][:, :, 512 * key[3]:512 * key[3] + 512]
             if key[0] == "b":
@@ -115,10 +117,12 @@ def tile_linearrecurrentunitcomplexeightstep_x1_kernel(tc, u, b, nu, theta, gamm
             else:
                 out = grouped[key][:].rearrange("p (t e m j) -> p e t m j", t=4, m=2, j=4)
                 in_ = half.rearrange("p j (e m t) -> p e t m j", m=2, t=4)
-            if eng == "V":
-                nc.vector.tensor_copy(out=out, in_=in_)
-            else:
-                nc.scalar.copy(out=out, in_=in_)
+            rows = out.shape[1] // pieces
+            for lo in range(0, out.shape[1], rows):
+                if eng == "V":
+                    nc.vector.tensor_copy(out=out[:, lo:lo + rows], in_=in_[:, lo:lo + rows])
+                else:
+                    nc.scalar.copy(out=out[:, lo:lo + rows], in_=in_[:, lo:lo + rows])
 
         def quant_w(key):
             codes[key] = const.tile([P, 512], U32, name="wc_" + "_".join([str(k) for k in key]), align_bytes=64)
@@ -279,13 +283,13 @@ def tile_linearrecurrentunitcomplexeightstep_x1_kernel(tc, u, b, nu, theta, gamm
                 in_=yb[g][:, 64 * h:64 * h + 64, :, :].rearrange("p n s t -> p (n s t)"))
             nc.sync.dma_start(out=out_1[g, :, 512 * h:512 * h + 512, :].rearrange("p m t -> p (m t)").bitcast(I32), in_=yq[g, h][:].bitcast(I32))
 
-        load_b(0, 0, 0)
+        load_b(0, 0, 0, 2)
         load_b(0, 1, 0)
-        load_u(0)
         load_b(1, 0, 0)
+        load_u(0)
         load_b(1, 1, 0)
         load_b(0, 0, 1)
-        interleave("V", ("b", 0, 0, 0))
+        interleave("V", ("b", 0, 0, 0), 2)
         load_b(0, 1, 1)
         interleave("S", ("b", 0, 1, 0))
         load_b(1, 0, 1)

import math
from contextlib import ExitStack

import concourse.mybir as mybir
from concourse.masks import make_identity

F32 = mybir.dt.float32
BF16 = mybir.dt.bfloat16
I32 = mybir.dt.int32
U32 = mybir.dt.uint32
U8 = mybir.dt.uint8
FP8X4 = mybir.dt.float8_e4m3fn_x4
ALU = mybir.AluOpType
ACT = mybir.ActivationFunctionType

NB, T, D, N = 128, 8, 1024, 1024
P = 128
FLOPS = 4 * 2 * NB * T * D * N

CHUNKS = ((0, 1), (2, 3), (4, 5), (6,), (7,))


def tile_linearrecurrentunitcomplexeightstep_x1_kernel(tc, u, b, nu, theta, gamma, c, d, out_0, out_1, out_2):
    nc = tc.nc
    with ExitStack() as ctx:
        const = ctx.enter_context(tc.tile_pool(name="const", bufs=1))
        pool = ctx.enter_context(tc.tile_pool(name="work", bufs=1))
        psum = ctx.enter_context(tc.psum_pool(name="psum", bufs=1))

        v4 = const.tile([P, 1024], BF16, name="v4", align_bytes=64)
        v4p = const.tile([P, 1024], BF16, name="v4p", align_bytes=64)
        nc.vector.memset(v4[:], 0.0)
        for i, vec in enumerate((nu, theta, gamma, d)):
            nc.scalar.dma_start(out=v4[i:i + 1, :], in_=vec.unsqueeze(0))
        warm = const.tile([P, 2], F32, name="warm")
        nc.vector.memset(warm[:], 0.0)
        nc.scalar.activation(out=warm[:, 1:2], in_=warm[:, 0:1], func=ACT.Exp)
        nc.gpsimd.memset(v4p[:], 0.0)
        ident32 = const.tile([P, P], F32, name="ident32")
        make_identity(nc, ident32[:])
        ident16 = const.tile([P, P], BF16, name="ident16")
        nc.gpsimd.tensor_copy(out=ident16[:], in_=ident32[:])

        u_nat = {}

        def load_u(ch):
            w = len(CHUNKS[ch])
            t0 = CHUNKS[ch][0]
            u_nat[ch] = pool.tile([P, w, D], BF16, name="u_nat", tag="u_nat", bufs=2, align_bytes=64)
            nc.sync.dma_start(out=u_nat[ch][:], in_=u[:, t0:t0 + w, :])

        raw = {}

        def load_b(part, g, G, pieces=1):
            raw["b", part, g, G] = pool.tile([P, 4, 512], BF16, name="raw_b", tag="raw_b", bufs=5, align_bytes=64)
            step = 512 // pieces
            for lo in range(0, 512, step):
                nc.sync.dma_start(
                    out=raw["b", part, g, G][:, :, lo:lo + step],
                    in_=b[part, 512 * g:512 * g + 512, 512 * G + lo:512 * G + lo + step].rearrange("(p j) w -> p j w", j=4))

        def load_c(part, G):
            raw["c", part, G] = pool.tile([P, 4, 1024], BF16, name="raw_c", tag="raw_c", bufs=2, align_bytes=64)
            for j in range(4):
                nc.sync.dma_start(
                    out=raw["c", part, G][:, j, :],
                    in_=c[part, 512 * G:512 * G + 512, :].rearrange("(q j i) w -> j q i w", j=4, i=8)[j])


        vecs = const.tile([P, 8, 4], F32, name="vecs")
        lam = const.tile([P, 3, 8], F32, name="lam")

        tmp = const.tile([P, 5, 8], F32, name="tmp")

        def const_a():
            nc.vector.tensor_copy(
                out=v4p[0:4, :].rearrange("p (G t q i) -> p G q t i", G=2, t=4, q=16),
                in_=v4[0:4, :].rearrange("p (G q t i) -> p G q t i", G=2, t=4, q=16))
            vp = psum.tile([P, 8, P], BF16, name="vp", tag="tr", bufs=2)
            for k in range(8):
                nc.tensor.transpose(vp[:, k, :], v4p[:, P * k:P * k + P], ident16[:])
            nc.vector.tensor_copy(out=vecs[:, :, 0:3], in_=vp[:, :, 0:3])
            dp = psum.tile([P, 8, P], BF16, name="dp", tag="tr", bufs=2)
            for k in range(8):
                g, t = divmod(k, 4)
                nc.tensor.transpose(dp[:, k, :], v4[:, 512 * g + t:512 * g + 512:4], ident16[:])
            nc.vector.tensor_copy(out=vecs[:, :, 3:4], in_=dp[:, :, 3:4])

            nc.vector.tensor_scalar(out=tmp[:, 2, :], in0=vecs[:, :, 1], scalar1=-1.0, scalar2=math.pi / 2, op0=ALU.mult, op1=ALU.add)

        def const_b():
            nc.scalar.activation(out=tmp[:, 0, :], in_=vecs[:, :, 0], func=ACT.Exp)
            nc.scalar.activation(out=tmp[:, 1, :], in_=tmp[:, 0, :], func=ACT.Exp, scale=-1.0)
            nc.scalar.activation(out=tmp[:, 3, :], in_=vecs[:, :, 1], func=ACT.Sin)
            nc.scalar.activation(out=tmp[:, 4, :], in_=tmp[:, 2, :], func=ACT.Sin)

        def const_c():
            nc.vector.tensor_tensor(out=lam[:, 0, :], in0=tmp[:, 1, :], in1=tmp[:, 4, :], op=ALU.mult)
            nc.vector.tensor_tensor(out=lam[:, 1, :], in0=tmp[:, 1, :], in1=tmp[:, 3, :], op=ALU.mult)
            nc.vector.tensor_scalar(out=lam[:, 2, :], in0=lam[:, 1, :], scalar1=-1.0, scalar2=None, op0=ALU.mult)

        LR, LI, NLI = range(3)

        def col(which, k):
            return lam[:, which, k:k + 1]

        grouped = {}
        codes = {}
        scales = {}

        def interleave(eng, key, pieces=1):
            grouped[key] = pool.tile([P, 2048], BF16, name="grouped", tag="grouped", bufs=3, align_bytes=64)
            half = raw[key][:] if key[0] == "b" else raw[key[:3]][:, :, 512 * key[3]:512 * key[3] + 512]
            if key[0] == "b":
                out = grouped[key][:].rearrange("p (t q i j) -> p q t i j", t=4, q=16, i=8)
                in_ = half.rearrange("p j (q t i) -> p q t i j", t=4, i=8)
            else:
                out = grouped[key][:].rearrange("p (t e m j) -> p e t m j", t=4, m=2, j=4)
                in_ = half.rearrange("p j (e m t) -> p e t m j", m=2, t=4)
            rows = out.shape[1] // pieces
            for lo in range(0, out.shape[1], rows):
                if eng == "V":
                    nc.vector.tensor_copy(out=out[:, lo:lo + rows], in_=in_[:, lo:lo + rows])
                else:
                    nc.scalar.copy(out=out[:, lo:lo + rows], in_=in_[:, lo:lo + rows])

        def quant_w(key):
            codes[key] = const.tile([P, 512], U32, name="wc_" + "_".join([str(k) for k in key]), align_bytes=64)
            scales[key] = const.tile([P, 512], U8, name="ws_" + "_".join([str(k) for k in key]), align_bytes=64)
            nc.vector.quantize_mx(out=codes[key][:].bitcast(FP8X4), scales=scales[key][:], in_=grouped[key][:])

        ug = {}
        uq = {}
        us = {}

        def u_transpose(ch):
            w = len(CHUNKS[ch])
            ug[ch] = const.tile([P, 2, w * P, 4], BF16, name="ug%d" % ch, align_bytes=64)
            words = u_nat[ch][:].rearrange("p w k -> p (w k)").bitcast(F32)
            for s in range(w):
                bank = psum.tile([P, 2, 2, P], F32, name="xt", tag="tr", bufs=2)
                for g in range(2):
                    for e in range(2):
                        lo = 512 * s + 256 * g
                        nc.tensor.transpose(bank[:, g, e, :], words[:, lo + e:lo + 256:2], ident32[:])
                nc.scalar.copy(
                    out=ug[ch][:, :, P * s:P * s + P, :].rearrange("p g n j -> p g (n j)").bitcast(F32).rearrange("p g (n e) -> p g n e", e=2),
                    in_=bank[:].rearrange("p g e n -> p g n e"))

        def u_quant(ch):
            w = len(CHUNKS[ch])
            uq[ch] = pool.tile([P, 2 * w * P], U32, name="uq", tag="uq", bufs=2, align_bytes=64)
            us[ch] = pool.tile([P, 2 * w * P], U8, name="us", tag="us", bufs=2, align_bytes=64)
            nc.vector.quantize_mx(out=uq[ch][:].bitcast(FP8X4), scales=us[ch][:], in_=ug[ch][:].rearrange("p g n j -> p (g n j)"))

        state = {}
        acc = {}

        def stage1(ch, n):
            w = len(CHUNKS[ch])
            G, t = divmod(n, 4)
            acc[ch, n] = psum.tile([P, 2, w * P], F32, name="acc", tag="acc", bufs=3)
            for part in range(2):
                for g in range(2):
                    key = ("b", part, g, G)
                    nc.tensor.matmul_mx(
                        out=acc[ch, n][:, part, :],
                        lhsT=codes[key][:, P * t:P * t + P].bitcast(FP8X4), lhsT_scale=scales[key][:, P * t:P * t + P],
                        rhs=uq[ch][:, w * P * g:w * P * (g + 1)].bitcast(FP8X4), rhs_scale=us[ch][:, w * P * g:w * P * (g + 1)],
                        start=(g == 0), stop=(g == 1))

        def drain(ch, n):
            w = len(CHUNKS[ch])
            G, t = divmod(n, 4)
            if (ch, G) not in state:
                state[ch, G] = pool.tile([P, 4, 2, w * P], F32, name="state", tag="state", bufs=4, align_bytes=64)
            nc.scalar.activation(out=state[ch, G][:, t, :, :], in_=acc[ch, n][:], func=ACT.Copy, scale=vecs[:, n, 2:3])

        def proj(ch, n):
            stage1(ch, n)
            drain(ch, n)

        def rec(ch, G, s):
            if s > 0:
                prev = state[ch, G][:, :, :, P * (s - 1):P * s]
            else:
                wp = len(CHUNKS[ch - 1])
                prev = state[ch - 1, G][:, :, :, P * (wp - 1):P * wp]
            cur = state[ch, G][:, :, :, P * s:P * s + P]
            for t in range(4):
                n = 4 * G + t
                nc.vector.scalar_tensor_tensor(out=cur[:, t, 0, :], in0=prev[:, t, 1, :], scalar=col(NLI, n), in1=cur[:, t, 0, :], op0=ALU.mult, op1=ALU.add)
                nc.vector.scalar_tensor_tensor(out=cur[:, t, 1, :], in0=prev[:, t, 0, :], scalar=col(LI, n), in1=cur[:, t, 1, :], op0=ALU.mult, op1=ALU.add)
            for t in range(4):
                nc.vector.scalar_tensor_tensor(out=cur[:, t, :, :], in0=prev[:, t, :, :], scalar=col(LR, 4 * G + t), in1=cur[:, t, :, :], op0=ALU.mult, op1=ALU.add)

        hb = {}
        hq = {}
        hs = {}

        def h_copy(eng, ch, G, part):
            w = len(CHUNKS[ch])
            if (ch, G) not in hb:
                hb[ch, G] = pool.tile([P, 2, w * P, 4], BF16, name="hb", tag="hb", bufs=3, align_bytes=64)
            out = hb[ch, G][:, part, :, :].rearrange("p (c i) t -> p c t i", i=4)
            in_ = state[ch, G][:, :, part, :].rearrange("p t (c i) -> p c t i", i=4)
            sign = 1.0 - 2.0 * part
            if eng == "V":
                nc.vector.tensor_scalar(out=out, in0=in_, scalar1=sign, scalar2=None, op0=ALU.mult)
            else:
                nc.scalar.activation(out=out, in_=in_, func=ACT.Copy, scale=sign)

        def h_quant(ch, G):
            w = len(CHUNKS[ch])
            hq[ch, G] = pool.tile([P, 2 * w * P], U32, name="hq", tag="hq", bufs=4, align_bytes=64)
            hs[ch, G] = pool.tile([P, 2 * w * P], U8, name="hs", tag="hs", bufs=4, align_bytes=64)
            nc.vector.quantize_mx(out=hq[ch, G][:].bitcast(FP8X4), scales=hs[ch, G][:], in_=hb[ch, G][:].rearrange("p r n t -> p (r n t)"))

        yp = {}
        ysb = {}
        yb = [const.tile([P, NB, T, 4], BF16, name="yb%d" % g, align_bytes=64) for g in range(2)]

        def stage2(ch, k):
            w = len(CHUNKS[ch])
            per = 4 // w
            if k % per == 0:
                yp[ch, k // per] = psum.tile([P, per, w * P], F32, name="yp", tag="yp", bufs=3)
            g, t = divmod(k, 4)
            for i in range(4):
                G, part = divmod(i, 2)
                key = ("c", part, G, g)
                nc.tensor.matmul_mx(
                    out=yp[ch, k // per][:, k % per, :],
                    lhsT=codes[key][:, P * t:P * t + P].bitcast(FP8X4), lhsT_scale=scales[key][:, P * t:P * t + P],
                    rhs=hq[ch, G][:, w * P * part:w * P * (part + 1)].bitcast(FP8X4), rhs_scale=hs[ch, G][:, w * P * part:w * P * (part + 1)],
                    start=(i == 0), stop=(i == 3))

        def skip_add(ch, k):
            w = len(CHUNKS[ch])
            per = 4 // w
            g, t = divmod(k, 4)
            if (ch, g) not in ysb:
                ysb[ch, g] = pool.tile([P, 4, w * P], F32, name="ysb", tag="ysb", bufs=4, align_bytes=64)
            nc.vector.scalar_tensor_tensor(
                out=ysb[ch, g][:, t, :], in0=ug[ch][:, g, :, t], scalar=vecs[:, k, 3:4], in1=yp[ch, k // per][:, k % per, :], op0=ALU.mult, op1=ALU.add)

        def y_round(eng, ch, g):
            w = len(CHUNKS[ch])
            t0 = CHUNKS[ch][0]
            out = yb[g][:, :, t0:t0 + w, :].rearrange("p (c i) s t -> p c s t i", i=4)
            in_ = ysb[ch, g][:].rearrange("p t (s c i) -> p c s t i", s=w, i=4)
            if eng == "V":
                nc.vector.tensor_copy(out=out, in_=in_)
            else:
                nc.scalar.copy(out=out, in_=in_)

        osb = {}

        def y_store(eng, ch, g, s):
            w = len(CHUNKS[ch])
            t = CHUNKS[ch][s]
            bank = psum.tile([P, 4, P], F32, name="ot", tag="tr", bufs=2)
            for k in range(4):
                nc.tensor.transpose(bank[:, k, :], ysb[ch, g][:, k, P * s:P * s + P], ident32[:])
            if (ch, s) not in osb:
                osb[ch, s] = pool.tile([P, D], F32, name="osb", tag="osb", bufs=3, align_bytes=64)
            out = osb[ch, s][:, 512 * g:512 * g + 512].rearrange("p (m t) -> p m t", t=4)
            in_ = bank[:].rearrange("p t m -> p m t")
            if eng == "V":
                nc.vector.tensor_copy(out=out, in_=in_)
            else:
                nc.scalar.copy(out=out, in_=in_)
            if g == 1:
                nc.sync.dma_start(out=out_0[:, t, :], in_=osb[ch, s][:])

        ysc = const.tile([P, 2, 1024], U8, name="ysc", align_bytes=64)
        yq = {}

        def plane(g, h):
            yq[g, h] = const.tile([P, 512], U32, name="yq%d%d" % (g, h), align_bytes=64)
            nc.vector.quantize_mx(
                out=yq[g, h][:].bitcast(FP8X4), scales=ysc[:, g, 512 * h:512 * h + 512],
                in_=yb[g][:, 64 * h:64 * h + 64, :, :].rearrange("p n s t -> p (n s t)"))
            nc.sync.dma_start(out=out_1[g, :, 512 * h:512 * h + 512, :].rearrange("p m t -> p (m t)").bitcast(I32), in_=yq[g, h][:].bitcast(I32))

        load_b(0, 0, 0, 2)
        load_b(0, 1, 0)
        load_b(1, 0, 0)
        load_u(0)
        load_b(1, 1, 0)
        load_b(0, 0, 1)
        interleave("V", ("b", 0, 0, 0), 2)
        load_b(0, 1, 1)
        interleave("S", ("b", 0, 1, 0))
        load_b(1, 0, 1)
        const_a()
        const_b()
        const_c()
        quant_w(("b", 0, 0, 0))
        u_transpose(0)
        interleave("V", ("b", 1, 0, 0))
        load_b(1, 1, 1)
        load_u(1)
        load_c(0, 0)
        load_c(1, 0)
        u_quant(0)
        quant_w(("b", 0, 1, 0))
        interleave("S", ("b", 1, 1, 0))
        quant_w(("b", 1, 0, 0))
        load_u(2)
        interleave("V", ("b", 0, 0, 1))
        quant_w(("b", 1, 1, 0))
        proj(0, 0)
        proj(0, 1)
        proj(0, 2)
        proj(0, 3)
        quant_w(("b", 0, 0, 1))
        interleave("V", ("b", 0, 1, 1))
        interleave("S", ("b", 1, 0, 1))
        rec(0, 0, 1)
        quant_w(("b", 0, 1, 1))
        interleave("V", ("b", 1, 1, 1))
        quant_w(("b", 1, 0, 1))
        u_transpose(1)
        load_u(3)
        quant_w(("b", 1, 1, 1))
        u_quant(1)
        h_copy("S", 0, 0, 0)
        h_copy("S", 0, 0, 1)
        proj(0, 4)
        proj(0, 5)
        proj(0, 6)
        proj(0, 7)
        proj(1, 0)
        proj(1, 1)
        proj(1, 2)
        proj(1, 3)
        interleave("V", ("c", 0, 0, 0))
        rec(0, 1, 1)
        quant_w(("c", 0, 0, 0))
        h_quant(0, 0)
        interleave("S", ("c", 0, 0, 1))
        load_c(0, 1)
        interleave("V", ("c", 1, 0, 0))
        rec(1, 0, 0)
        rec(1, 0, 1)
        quant_w(("c", 1, 0, 0))
        h_copy("S", 0, 1, 0)
        h_copy("S", 0, 1, 1)
        proj(1, 4)
        proj(1, 5)
        proj(1, 6)
        proj(1, 7)
        u_transpose(2)
        load_u(4)
        quant_w(("c", 0, 0, 1))
        interleave("S", ("c", 1, 0, 1))
        load_c(1, 1)
        u_quant(2)
        quant_w(("c", 1, 0, 1))
        h_copy("S", 1, 0, 0)
        h_copy("S", 1, 0, 1)
        interleave("V", ("c", 0, 1, 0))
        rec(1, 1, 0)
        rec(1, 1, 1)
        quant_w(("c", 0, 1, 0))
        h_quant(0, 1)
        interleave("S", ("c", 0, 1, 1))
        h_quant(1, 0)
        interleave("V", ("c", 1, 1, 0))
        proj(2, 0)
        proj(2, 1)
        proj(2, 2)
        proj(2, 3)
        quant_w(("c", 0, 1, 1))
        quant_w(("c", 1, 1, 0))
        interleave("S", ("c", 1, 1, 1))
        rec(2, 0, 0)
        rec(2, 0, 1)
        quant_w(("c", 1, 1, 1))
        stage2(0, 0)
        stage2(0, 1)
        stage2(0, 2)
        stage2(0, 3)
        h_copy("S", 1, 1, 0)
        h_copy("S", 1, 1, 1)
        skip_add(0, 0)
        skip_add(0, 1)
        skip_add(0, 2)
        skip_add(0, 3)
        stage2(0, 4)
        stage2(0, 5)
        stage2(0, 6)
        stage2(0, 7)
        skip_add(0, 4)
        skip_add(0, 5)
        skip_add(0, 6)
        skip_add(0, 7)
        proj(2, 4)
        proj(2, 5)
        proj(2, 6)
        proj(2, 7)
        h_copy("S", 2, 0, 0)
        h_copy("S", 2, 0, 1)
        h_quant(1, 1)
        y_round("S", 0, 0)
        y_store("S", 0, 0, 0)
        y_store("S", 0, 0, 1)
        stage2(1, 0)
        stage2(1, 1)
        stage2(1, 2)
        stage2(1, 3)
        rec(2, 1, 0)
        rec(2, 1, 1)
        u_transpose(3)
        u_quant(3)
        proj(3, 0)
        proj(3, 1)
        proj(3, 2)
        proj(3, 3)
        skip_add(1, 0)
        skip_add(1, 1)
        skip_add(1, 2)
        skip_add(1, 3)
        stage2(1, 4)
        stage2(1, 5)
        stage2(1, 6)
        stage2(1, 7)
        h_quant(2, 0)
        y_round("S", 0, 1)
        y_store("S", 0, 1, 0)
        y_store("S", 0, 1, 1)
        skip_add(1, 4)
        skip_add(1, 5)
        skip_add(1, 6)
        skip_add(1, 7)
        h_copy("S", 2, 1, 0)
        h_copy("S", 2, 1, 1)
        rec(3, 0, 0)
        proj(3, 4)
        proj(3, 5)
        proj(3, 6)
        proj(3, 7)
        h_copy("S", 3, 0, 0)
        h_copy("S", 3, 0, 1)
        h_quant(2, 1)
        y_round("S", 1, 0)
        y_store("S", 1, 0, 0)
        y_store("S", 1, 0, 1)
        stage2(2, 0)
        stage2(2, 1)
        stage2(2, 2)
        stage2(2, 3)
        rec(3, 1, 0)
        u_transpose(4)
        u_quant(4)
        proj(4, 0)
        proj(4, 1)
        proj(4, 2)
        proj(4, 3)
        skip_add(2, 0)
        skip_add(2, 1)
        skip_add(2, 2)
        skip_add(2, 3)
        stage2(2, 4)
        stage2(2, 5)
        stage2(2, 6)
        stage2(2, 7)
        h_quant(3, 0)
        y_round("S", 1, 1)
        y_store("S", 1, 1, 0)
        y_store("S", 1, 1, 1)
        skip_add(2, 4)
        skip_add(2, 5)
        skip_add(2, 6)
        skip_add(2, 7)
        h_copy("S", 3, 1, 0)
        h_copy("S", 3, 1, 1)
        rec(4, 0, 0)
        proj(4, 4)
        proj(4, 5)
        proj(4, 6)
        proj(4, 7)
        h_copy("S", 4, 0, 0)
        h_copy("S", 4, 0, 1)
        h_quant(3, 1)
        y_round("S", 2, 0)
        y_store("S", 2, 0, 0)
        y_store("S", 2, 0, 1)
        stage2(3, 0)
        stage2(3, 1)
        stage2(3, 2)
        stage2(3, 3)
        rec(4, 1, 0)
        skip_add(3, 0)
        skip_add(3, 1)
        skip_add(3, 2)
        skip_add(3, 3)
        stage2(3, 4)
        stage2(3, 5)
        stage2(3, 6)
        stage2(3, 7)
        h_quant(4, 0)
        y_round("S", 2, 1)
        y_store("S", 2, 1, 0)
        y_store("S", 2, 1, 1)
        skip_add(3, 4)
        skip_add(3, 5)
        skip_add(3, 6)
        skip_add(3, 7)
        h_copy("S", 4, 1, 0)
        h_copy("S", 4, 1, 1)
        h_quant(4, 1)
        y_round("S", 3, 0)
        y_store("S", 3, 0, 0)
        stage2(4, 0)
        stage2(4, 1)
        stage2(4, 2)
        stage2(4, 3)
        y_round("S", 3, 1)
        y_store("S", 3, 1, 0)
        skip_add(4, 0)
        skip_add(4, 1)
        skip_add(4, 2)
        skip_add(4, 3)
        stage2(4, 4)
        stage2(4, 5)
        stage2(4, 6)
        stage2(4, 7)
        y_round("S", 4, 0)
        y_store("S", 4, 0, 0)
        skip_add(4, 4)
        skip_add(4, 5)
        skip_add(4, 6)
        skip_add(4, 7)
        y_round("S", 4, 1)
        y_store("S", 4, 1, 0)
        plane(0, 0)
        plane(0, 1)
        plane(1, 0)
        plane(1, 1)

        for q in range(4):
            nc.sync.dma_start(
                out=out_2[:, 4 * q:4 * q + 4, :].bitcast(I32).rearrange("g r m -> r g m"),
                in_=ysc[32 * q:32 * q + 4, :, :].bitcast(I32))
